import numpy as np, ml_dtypes
CORES = [3,7,11,15,131,135,139,143]
N = 8
BF = ml_dtypes.bfloat16
W, L, S, T, HS, AS = 2048, 256, 8, 2, 1, 3
def parts(rng):
    D = rng.integers(0, W, (N, 8, 16, W)); one = rng.integers(0, W, (N, 8, 1, W))
    D = np.where((rng.random((N, 8, 1, W)) < 0.5) & (rng.random(D.shape) < 0.5), one, D)
    D = np.where(rng.random(D.shape) < 0.25, S * rng.integers(0, L, D.shape) + rng.integers(0, T, D.shape), D)
    X = rng.integers(0, 256, (N, 8, 16, W)); th = rng.integers(1000, 1800, (N, 8, 16))
    n = np.array([1, 1, 2, 2, 4, 4, 16, 16])[np.argsort(rng.random((N, 8)), axis=1)]
    j = (np.arange(16)[None, None, :] % n[:, :, None])[..., None]
    ti = np.take_along_axis(np.argsort(rng.random((N, 8, 16, 16)), axis=-1)[..., :3], j, 2)
    sg = np.take_along_axis(2 * rng.integers(0, 2, (N, 8, 16, 3)) - 1, j, 2)
    return D, X, th, ti, sg
def pack(D, X, th, ti, sg):
    return {"dg": np.ascontiguousarray(D.reshape(N, 128, W)).astype(np.int32), "xv": np.ascontiguousarray(X.reshape(N, 128, W)).astype(np.float32).astype(BF),
            "th": np.ascontiguousarray(th.reshape(N, 128, 1)).astype(np.int32), "ti": np.ascontiguousarray(ti.reshape(N, 128, 3)).astype(np.int32), "sg": np.ascontiguousarray(sg.reshape(N, 128, 3)).astype(np.int32)}
def setup_inputs(rng):
    return pack(*parts(rng))
def setup_inputs_corners(rng):
    D, X, th, ti, sg = parts(rng); c = np.arange(W)[None, :]; base = int(rng.integers(0, N)); o = rng.permutation(8)
    th = rng.choice(np.array([0, 1, 1365, 4080, 4081, 4081]), th.shape)
    for q in range(N):
        for g in range(8):
            m = int(o[g])
            if m == 0: D[q, g] = c
            if m == 1: D[q, g] = rng.choice(np.array([0, W - 1]), (16, W))
            if m == 2: D[q, g] = (c + 1 + np.arange(16)[:, None]) % W; th[q, g] = 4081
            if m == 3: D[q, g] = S * rng.integers(0, L, (16, W)) + rng.integers(0, T, (16, W))
            if m == 4: D[q, g] = rng.integers(0, W, (1, W)); th[q, g] = 4081
            if m == 5: D[q, g] = (c - 1) % W; th[q, g] = 0
            if m == 6: D[q, g] = rng.integers(0, W // 2, (16, W)) + (W // 2) * int(rng.integers(0, 2)); th[q, g] = 4081
            if m == 7: th[q, g] = 4080
    k = rng.random((N, 8, 1, W)); X = np.where(k < 0.1, 0, np.where(k < 0.2, 255, X))
    for q in (base % N, (base + 1) % N):
        for t in range(T): X[q, :, :, t::S] = 255
    a = (base + 2) % N; b = (base + 3) % N
    sg[a, :, :, 0] = -sg[a, :, :, 1]; sg[b] = sg[b][:, :, :1]
    return pack(D, X, th, ti, sg)
def setup_inputs_ties(rng):
    D, X, th, ti, sg = parts(rng)
    pr = rng.integers(0, 256, (8, 16, 24))
    pr[..., 12:] = np.minimum(pr[..., :12] + (np.arange(16)[None, :, None] == rng.integers(0, 16, (8, 1, 12))), 255)
    X = np.take_along_axis(np.broadcast_to(pr, (N, 8, 16, 24)), rng.integers(0, 24, (N, 8, 1, W)), 3)
    dd = np.add.reduce(np.abs(pr[:, :, :, None] - pr[:, :, None, :]), axis=1)
    th = dd[np.arange(8)[None, :, None], rng.integers(0, 24, (N, 8, 16)), rng.integers(0, 24, (N, 8, 16))] + rng.integers(0, 2, (N, 8, 16))
    return pack(D, X, th, ti, sg)
def setup_inputs_spread(rng):
    D, X, th, ti, sg = parts(rng)
    X = np.minimum((np.exp2(8 * rng.random((N, 8, 1, W))) * rng.random(X.shape)).astype(np.int64), 255)
    e = rng.choice(np.array([1, 2, 4]), (N, 8, 16, 1)); u = rng.random(D.shape)
    D = np.minimum((W * np.where(e == 1, u, np.where(e == 2, u * u, u * u * u * u))).astype(np.int64), W - 1)
    D = np.where(rng.random((N, 8, 16, 1)) < 0.5, D, W - 1 - D)
    th = np.minimum(np.exp2(12 * rng.random(th.shape)).astype(np.int64), 4081)
    return pack(D, X, th, ti, sg)
def setup_inputs_ends(rng):
    D, X, th, ti, sg = parts(rng)
    k = rng.random((N, 8, 1, W)); D = np.where(k < 0.4, (W - 1) * rng.integers(0, 2, k.shape), np.where(k < 0.75, (W - 1) * rng.integers(0, 2, D.shape), D))
    k = rng.random((N, 8, 1, W)); X = 255 * np.where(k < 0.3, rng.integers(0, 2, k.shape), rng.integers(0, 2, X.shape))
    th = 4081 * rng.integers(0, 2, th.shape); th[:, 0, 0] = 0; th[:, 7, 15] = 4081
    low = np.zeros((N, 8, 16, 1), np.int64); mid = rng.integers(1, 15, (N, 8, 16, 1))
    low[:, 4] = 1; mid[:, 4] = rng.integers(2, 15, (N, 16, 1))
    mid[:, 7] = 1 + np.arange(16).reshape(16, 1) % 14
    ti = np.concatenate([low, np.full((N, 8, 16, 1), 15), mid], axis=-1)
    ti = np.take_along_axis(ti, np.argsort(rng.random(ti.shape), axis=-1), 3)
    for q in (N - 2, N - 1, 0):
        c = (W - 1) * rng.integers(0, 2, (8, 1, L)); z = 255 * rng.integers(0, 2, (8, 1, L))
        c[..., 0] = 0; c[..., 1] = W - 1; c[..., L - 1] = W - 1; z[..., 0] = 0; z[..., 1] = 0; z[..., L - 1] = 0
        far = ((c == 0) == (z == 255)) & (rng.random((8, 1, L)) < 0.5); far[..., 0] = False; far[..., L - 1] = False
        off = (rng.integers(0, 16, (8, 16, L)) >> (3 * rng.integers(0, 2, (8, 1, L)))) * far
        x = np.abs(z - off)
        if q == N - 2:
            u = rng.permutation(8 * (L - 2))[:19 + 2 * int(rng.integers(0, 50))]; a = u // (L - 2); i = 1 + u % (L - 2)
            h = 255 * rng.integers(0, 2, (len(u), 16)); h[:, :2] = 0; h[:, 15] = 255
            c[a, 0, i] = W - 1; x[a, :, i] = h
        D[q, :, :, 0::S] = c; X[q, :, :, 0::S] = x
    for q in (N - 2, N - 1, 0, 1):
        D[q, :, :, 0] = 0; D[q, :, :, W - 1] = W - 1; X[q, :, :, 0] = 0; X[q, :, :, W - 1] = 255
    for q in (N - 1, 0):
        sg[q] = sg[q][:, :, :1]; sg[q, :, 0] = 1; sg[q, :, 15] = -1
    sg[1, :, :, 0] = -sg[1, :, :, 1]
    return pack(D, X, th, ti, sg)
def check_inputs(d):
    bad = []
    for k, lo, hi in (("dg", 0, W - 1), ("xv", 0, 255), ("th", 0, 4081), ("ti", 0, 15), ("sg", -1, 1)):
        a = np.asarray(d[k]).astype(np.float64)
        if not (np.min(a) >= lo and np.max(a) <= hi): bad.append("range of " + k)
    a = np.asarray(d["xv"]).astype(np.float64)
    if not np.all(a == np.floor(a)): bad.append("whole numbers in xv")
    a = np.asarray(d["ti"])
    if np.any(a[..., 0] == a[..., 1]) or np.any(a[..., 0] == a[..., 2]) or np.any(a[..., 1] == a[..., 2]): bad.append("different rows in a triple of ti")
    if np.any(np.asarray(d["sg"]) == 0): bad.append("no zero in sg")
    return bad
def reference(dg, xv, th, ti, sg):
    D = dg.astype(np.int64).reshape(N, 8, 16, W); X = xv.astype(np.float32).astype(np.int32).reshape(N, 8, 16, W); H = th.astype(np.int64).reshape(N, 8, 16, 1)
    G = np.zeros((N, 8, 16, 16), np.int64); np.put_along_axis(G, ti.astype(np.int64).reshape(N, 8, 16, 3), sg.astype(np.int64).reshape(N, 8, 16, 3), 3)
    def dist(q, E, x):
        y = np.take_along_axis(X[q], E.reshape(8, 1, 16 * L), 2).reshape(8, 16, 16, L)
        return np.add.reduce(np.abs(y - x[:, :, None, :]), axis=1).astype(np.int64)
    for t in range(T):
        v = S * np.arange(L) + t; new = np.array(D); last = []
        for r in range(N):
            s = (r + 1 + t) % N; x = X[r][:, :, v]; E = D[r][:, :, v]; go = np.ones((8, 16, L), bool)
            for step in range(HS + AS):
                q = r if step < HS else s
                n = np.take_along_axis(D[q], E, 2)
                go = go & (dist(q, n, x) < H[q]); E = np.where(go, n, E)
            d = dist(s, E, x); b = np.where(np.take_along_axis(X[s], E, 2) > x, 1, -1)
            cyc = np.abs(np.matmul(G[s], b)) == 3
            charged = np.matmul(np.abs(G[s]).transpose(0, 2, 1), cyc.astype(np.int64)) > 0
            A = int(np.count_nonzero(np.any(cyc, axis=1)))
            keep = np.argmin(np.where(charged, d, 2 ** 20), axis=1)
            gone = charged & (np.arange(16)[None, :, None] != keep[:, None, :])
            new[r][:, :, v] = np.where(gone, (37 * E + d + A) & (W - 1), D[r][:, :, v]); last.append(E)
        D = new
    yd = np.concatenate([D[:, :, :, t::S] for t in range(T)], axis=3)
    return {"yd": yd.reshape(N, 128, T * L).astype(np.float32), "ye": np.stack(last).reshape(N, 128, L).astype(np.float32)}

@@ -1,0 +1,636 @@
+from concourse.bass import DstId, RemoteDMATransfer
+from concourse.mybir import dt, AluOpType, AxisListType, ActivationFunctionType
+
+W, L, S, N = 2048, 256, 8, 8
+NCH = 4
+LC = L // NCH
+CW = 16 * LC
+ALPHA = 60.0
+MID = 1023.5
+BIGP = 8192.0
+AL = AluOpType
+AF = ActivationFunctionType
+
+U_ = ["L0a", "L0b", "L0i", "LEa", "LEb", "LEi", "L1_0", "L1_1", "ndo", "ndi", "nd2"] + ["%s_%d" % (n, t) for n in ("L2", "L3", "L4", "LF") for t in (0, 1)]
+H_ = ["e0a", "e0b", "d0i"] + ["%s_%d" % (n, t) for n in ("h1", "m1", "g1", "h2", "h3", "h4", "hF", "m2", "m3", "m4") for t in (0, 1)]
+F_ = ["d0f", "dS_0", "dS_1", "mq", "q", "ga", "yd0", "yd1", "yef", "ndf", "ndg"] + ["ln%d_%d" % (k, t) for k in (2, 3, 4) for t in (0, 1)]
+B_ = ["x0", "xi", "r1a", "r1b", "r1i", "any"] + ["%s_%d" % (n, t) for n in ("r2", "r3", "r4", "bs", "sq", "ch", "go") for t in (0, 1)]
+I_ = ["qi", "ni"]
+POOLS = {"PU": (U_, "uint16"), "PH": (H_, "float16"), "PF": (F_, "float32"), "PB": (B_, "bfloat16"), "PI": (I_, "int32")}
+SLOT = {}
+SCRATCH = {}
+for _p in POOLS:
+    _names, _dt = POOLS[_p]
+    SCRATCH[_p] = ("sbuf", [128, 256 * len(_names)], _dt)
+    for _k, _n in enumerate(_names):
+        SLOT[_n] = (_p, 256 * _k)
+SCRATCH.update({
+    "dgs": ("sbuf", [128, W], "int32"), "dgf": ("sbuf", [128, W], "float32"), "xs": ("sbuf", [128, W], "bfloat16"),
+    "dcod": ("sbuf", [128, W], "bfloat16"), "xs2": ("sbuf", [128, W], "bfloat16"), "code2": ("sbuf", [128, W], "bfloat16"),
+    "xr0": ("sbuf", [128, 16 * L], "bfloat16"), "xr1": ("sbuf", [128, 16 * L], "bfloat16"), "xrn": ("sbuf", [128, 16 * L], "bfloat16"),
+    "zb": ("sbuf", [128, 32 * L], "bfloat16"), "ab": ("sbuf", [128, 32 * L], "bfloat16"), "gb": ("sbuf", [128, 32 * L], "bfloat16"),
+    "gh": ("sbuf", [128, 16 * L], "float16"),
+    "selb": ("sbuf", [128, 2048], "bfloat16"), "seln": ("sbuf", [128, 2048], "bfloat16"), "edb": ("sbuf", [128, 2048], "bfloat16"), "edh": ("sbuf", [128, 2048], "float16"),
+    "onb": ("sbuf", [128, 256], "bfloat16"), "onf": ("sbuf", [128, 256], "float32"), "on16": ("sbuf", [128, 128], "float32"),
+    "idb": ("sbuf", [128, 128], "bfloat16"), "idh": ("sbuf", [128, 128], "float16"), "idn": ("sbuf", [128, 128], "float16"),
+    "id37": ("sbuf", [128, 128], "float16"), "idp": ("sbuf", [128, 128], "bfloat16"), "idf": ("sbuf", [128, 128], "float32"),
+    "blk0": ("sbuf", [128, 128], "bfloat16"), "blk": ("sbuf", [128, 128], "bfloat16"),
+    "dupf": ("sbuf", [128, 256], "float32"), "dupb": ("sbuf", [128, 256], "bfloat16"), "iop": ("sbuf", [128, 256], "float32"),
+    "prow": ("sbuf", [128, 256], "bfloat16"), "rst": ("sbuf", [128, 256], "float32"),
+    "pm": ("sbuf", [128, 512], "float32"), "eq": ("sbuf", [128, 256], "bfloat16"),
+    "iq": ("sbuf", [128, 128], "float32"), "thi": ("sbuf", [128, 4], "int32"), "tii": ("sbuf", [128, 4], "int32"), "sgi": ("sbuf", [128, 4], "int32"),
+    "tif": ("sbuf", [128, 4], "float32"), "sgf": ("sbuf", [128, 4], "float32"),
+    "gq": ("sbuf", [128, 512], "float32"), "gj": ("sbuf", [128, 128], "bfloat16"),
+    "pk": ("sbuf", [128, 256], "bfloat16"), "pk2": ("sbuf", [128, 256], "bfloat16"),
+    "pt": ("sbuf", [128, 4], "float32"), "pt2": ("sbuf", [128, 4], "float32"),
+    "asum": ("sbuf", [128, 8], "float32"), "acol": ("sbuf", [128, 8], "float32"),
+})
+for _k in range(8):
+    SCRATCH["bank%d" % _k] = ("psum", [128, 512], "float32")
+SEMAPHORES = ["cv", "cs", "cp", "cg", "lsem", "ltab", "rx", "rtab", "rpk", "rpt", "rnh", "rn2"] + ["re%d" % c for c in range(NCH)] + ["ld%d" % k for k in range(10)]
+
+CY = 0.83e-3 * 1.2
+RELU = {(1, 0), (1, 1), (5, 3)}
+SG1 = ((1, 2, 3), (1, 2, 3))
+GC = 1.5
+HOP = 2.5
+
+
+def rank_program(g, core, T, topo):
+    rank = T.rank_of(core)
+    if rank is None:
+        return
+    cores = T.cores
+    ops, lastw, readers, tiles, own = [], {}, {}, [], {}
+    bankof = {}
+    cur = [0]
+    ENG = {"v": g.vector, "s": g.scalar, "p": g.tensor, "g": g, "y": g.sync}
+    CSEM = {"v": "cv", "s": "cs", "p": "cp", "g": "cg"}
+
+    def add(eng, dur, fn, r=(), w=(), ps=(), sem=None, inc=1, lat=0.0, extra=(), boost=0.0):
+        k = len(ops)
+        deps = set(extra)
+        keys_w = list(w) + [("ps", t) for t in ps]
+        for x in r:
+            if x in lastw:
+                deps.add(lastw[x])
+        for x in keys_w:
+            if x in lastw:
+                deps.add(lastw[x])
+            deps.update(readers.get(x, ()))
+        for x in r:
+            readers.setdefault(x, []).append(k)
+        for x in keys_w:
+            lastw[x] = k
+            readers[x] = []
+        deps.discard(k)
+        hard = set(extra)
+        for x in list(r) + list(w):
+            hard.update(own.get(("w", x), ()))
+        for x in w:
+            hard.update(own.get(("r", x), ()))
+            own.setdefault(("w", x), []).append(k)
+        for x in r:
+            own.setdefault(("r", x), []).append(k)
+        soft = set(d for d in deps if ops[d]["e"] == eng and d not in hard and ps)
+        ops.append({"e": eng, "d": dur, "f": fn, "deps": deps, "ps": list(ps), "sem": sem, "inc": inc, "lat": lat, "c": cur[0], "soft": soft, "n": keys_w[0] if keys_w else "-"})
+        for t in ps:
+            tiles[t].append(k)
+        return k
+
+    def tile():
+        tiles.append([])
+        return len(tiles) - 1
+
+    def ps(t):
+        return T["bank%d" % bankof[t]]
+
+    def rng(c):
+        if c is None:
+            return 0, L
+        if c < 0:
+            h = -1 - c
+            return 128 * h, 128 * h + 128
+        return LC * c, LC * c + LC
+
+    def A(name, c=None):
+        p, o = SLOT[name]
+        a, b = rng(c)
+        return T[p][:, o + a:o + b]
+
+    def K(name, c=None):
+        a, b = rng(c)
+        return [(name, k) for k in range(a // LC, b // LC)]
+
+    def nn(c):
+        a, b = rng(c)
+        return b - a
+
+    def vt(n, f):
+        return 0.04 + max(64, n * f) * CY
+
+    def vcopy(out, in_, n, f, r, w, p=()):
+        return add("v", vt(n, f), lambda: g.vector.tensor_copy(R(out), R(in_)), r, w, p)
+
+    def R(x):
+        return x[0]() if isinstance(x, tuple) else x
+
+    def vts(out, in0, s1, s2, o0, o1, n, f, r, w, p=()):
+        def em():
+            i0 = R(in0)
+            if o1 is None:
+                return g.vector.tensor_scalar(out, i0, s1, None, o0)
+            return g.vector.tensor_scalar(out, i0, s1, s2, o0, o1)
+        return add("v", vt(n, f), em, r, w, p)
+
+    def vtt(out, in0, in1, op, n, f, r, w, p=()):
+        return add("v", vt(n, f), lambda: g.vector.tensor_tensor(out, R(in0), R(in1), op), r, w, p)
+
+    def sact(out, in_, func, n, r, w, p=(), bias=0.0, scale=1.0, acc=None):
+        def em():
+            i0 = R(in_)
+            if acc is not None:
+                return g.scalar.activation(out, i0, func, bias=bias, scale=scale, accum_out=acc)
+            return g.scalar.activation(out, i0, func, bias=bias, scale=scale)
+        return add("s", 0.08 + n * CY, em, r, w, p)
+
+    def mm(lst, cyc, r, p):
+        def em():
+            out = None
+            for (a, b, lhs, rhs, st, sp) in lst:
+                out = g.tensor.matmul(ps(p)[:, a:b], lhs, rhs, st, sp)
+            return out
+        return add("p", 0.03 + cyc * 0.6e-3, em, r, (), (p,))
+
+    def load(eng, buf, src, sem, lat):
+        q = g.sync if eng == "y" else g.scalar
+        return add(eng, 0.1, lambda: q.dma_start(buf, src), (), [(sem, "ld")], (), sem, 16, lat)
+
+    load("y", T.dgs[:, :], T.dg[:, :], "ld1", 7.0)
+    load("y", T.xs[:, :], T.xv[:, :], "ld0", 9.0)
+    load("y", T.thi[:, 0:1], T.th[:, :], "ld4", 9.5)
+    load("y", T.tii[:, 0:3], T.ti[:, :], "ld2", 9.5)
+    load("y", T.sgi[:, 0:3], T.sg[:, :], "ld3", 9.5)
+    KX, KDG = ("ld0", "ld"), ("ld1", "ld")
+
+    add("v", vt(256, 0.5), lambda: g.vector.memset(T.onb[:, :], 1.0), (), ["onb"])
+    add("v", vt(256, 1), lambda: g.vector.memset(T.onf[:, :], 1.0), (), ["onf"])
+    add("v", vt(2048, 0.5), lambda: g.vector.memset(T.edb[:, :], 0.0), (), ["edb0"])
+    add("v", vt(2048, 0.5), lambda: g.vector.memset(T.selb[:, :], 0.0), (), ["selb0"])
+    add("g", 0.4, lambda: g.affine_select(T.idb[:, :], T.onb[:, 0:128], [[-1, 128]], AL.is_equal, 0.0, 0, 1), ["onb"], ["idb"])
+    add("g", 0.4, lambda: g.affine_select(T.blk0[:, :], T.onb[:, 0:128], [[-16, 8], [0, 16]], AL.is_ge, 0.0, 0, 1), ["onb"], ["blk0"])
+    add("g", 0.4, lambda: g.affine_select(T.blk[:, :], T.blk0[:, :], [[16, 8], [0, 16]], AL.is_ge, 0.0, 15, -1), ["blk0"], ["blk"])
+    add("g", 0.4, lambda: g.iota(T.iq[:, :], [[0, 8], [1, 16]], 0, 0, allow_small_or_imprecise_dtypes=True), (), ["iq"])
+    add("g", 0.6, lambda: g.affine_select(T.dupf[:, :], T.onf[:, :], [[-16, 8], [0, 2], [-1, 16]], AL.is_equal, 0.0, 0, 1), ["onf"], ["dupf"])
+    add("g", 0.6, lambda: g.iota(T.iop[:, :], [[0, 8], [0, 2], [1, 16]], 0, 0, allow_small_or_imprecise_dtypes=True), (), ["iop"])
+    for p in range(16):
+        def cp(p=p):
+            return g.vector.tensor_copy(T.edb[:, p * 128 + p:(p + 1) * 128:16], T.idb[:, p:128:16])
+        add("v", vt(8, 1), cp, ["idb", "edb0"], [("edb", p)])
+    KED = [("edb", p) for p in range(16)]
+    vcopy(T.edh[:, :], T.edb[:, :], 2048, 0.5, KED, ["edh"])
+    for p in range(16):
+        def cp2(p=p):
+            return g.scalar.activation(T.selb[:, p * 128 + p:(p + 1) * 128:16], T.blk[:, 0:128:16], AF.Copy)
+        add("s", 0.08 + 8 * CY, cp2, ["blk", "selb0"], [("selb", p)])
+    KSEL = [("selb", p) for p in range(16)]
+    if RELU:
+        vts(T.seln[:, :], T.selb[:, :], -1.0, None, AL.mult, None, 2048, 0.5, KSEL, ["seln"])
+    vcopy(T.idh[:, :], T.idb[:, :], 128, 0.5, ["idb"], ["idh"])
+    vts(T.idn[:, :], T.idb[:, :], -1.0, None, AL.mult, None, 128, 0.5, ["idb"], ["idn"])
+    vts(T.id37[:, :], T.idb[:, :], 37.0, None, AL.mult, None, 128, 0.5, ["idb"], ["id37"])
+    vts(T.idp[:, :], T.idb[:, :], BIGP, None, AL.mult, None, 128, 0.5, ["idb"], ["idp"])
+
+    def xrep(buf, src, rk, engs):
+        keys = []
+        for p in range(16):
+            e = engs[p % len(engs)]
+            o = T[buf][:, p:16 * L:16]
+            key = (buf, p)
+            keys.append(key)
+            if e == "v":
+                vcopy(o, src, 256, 0.5, rk, [key])
+            else:
+                sact(o, src, AF.Copy, 256, rk, [key])
+        return keys
+
+    xr0k = xrep("xr0", T.xs[:, 0:W:S], [KX], "vs")
+    vcopy(A("x0"), T.xs[:, 0:W:S], 256, 0.5, [KX], K("x0"))
+    vcopy(A("L0a"), T.dgs[:, 0:W:S], 256, 1, [KDG], K("L0a"))
+    vcopy(A("e0a"), A("L0a"), 256, 0.5, K("L0a"), K("e0a"))
+
+    vcopy(T.tif[:, 0:3], T.tii[:, 0:3], 3, 1, [("ld2", "ld")], ["tif"])
+    vcopy(T.sgf[:, 0:3], T.sgi[:, 0:3], 3, 1, [("ld3", "ld")], ["sgf"])
+    vcopy(T.pt[:, 0:1], T.thi[:, 0:1], 1, 1, [("ld4", "ld")], ["pth"])
+
+    def dest(r):
+        return cores[r % N]
+
+    def send(dsts, names_in, names_out, sem, dur, rd, after=(), lsem="lsem"):
+        trs, tot = [], 0
+        pieces = len(names_in)
+        for k in range(pieces):
+            d = dsts[k]
+            rid, pid = topo.addr(d, core)
+            es = topo.engines(core, d)
+            n = 1
+            while 2 * n * pieces <= min(len(es), 8):
+                n *= 2
+            m = sum(1 << e for e in es[k * n:(k + 1) * n])
+            trs.append((DstId(rid=rid, pnc=pid), m, names_in[k], names_out[k], sem[k]))
+            tot += n
+        if lsem == "lsem":
+            cnt["l"] += tot
+
+        def em():
+            return g.remote_dma_fused([RemoteDMATransfer(dst_ids=[a], dma_engine_mask=m, remote_sem=T.sem[s_], src=i, dst=o)
+                                       for (a, m, i, o, s_) in trs], local_sem=T.sem[lsem])
+        return add("g", dur, em, rd, (), (), "-", 0, 0.0, after)
+
+    cnt = {"l": 0}
+
+    def recv(sem, val, lat, after, keys):
+        return add("n", 0.0, None, (), keys, (), sem, val, lat, [after])
+
+    s1 = dest(rank + 1)
+    k = send([s1, s1], [A("x0"), A("L0a")], [A("xi"), A("L0i")], ["rx", "rx"], 1.5, K("x0") + K("L0a"))
+    recv("rx", 8, HOP, k, K("xi") + K("L0i"))
+
+    par = {}
+
+    def bufpair(buf, c):
+        n = par.get((buf, c), 0)
+        par[(buf, c)] = n + 1
+        o = (n % 2) * 16 * L + c * CW
+        return o, (buf, n % 2, c)
+
+    GT_ = 0.06 + CW * GC * CY
+
+    def diag(src, key, ed, kd, p, off=0, o0=0):
+        mm([(off, off + LC, ed[:, q * 128:(q + 1) * 128], src[:, o0 + q:o0 + CW:16], q == 0, q == 15) for q in range(16)], CW, [key] + kd, p)
+
+    def view(X, kx, lst, kl, xr, kxr, c, st):
+        zo, zk = bufpair("zb", c)
+        add("v", GT_, lambda: g.vector.tensor_tensor(T.zb[:, zo:zo + CW], X[:, :].indirect(lst), xr[:, c * CW:(c + 1) * CW], AL.subtract),
+            [kx] + kl + kxr, [zk])
+        ao, ak = bufpair("ab", c)
+        if (st, c) in RELU:
+            vts(T.ab[:, ao:ao + CW], T.zb[:, zo:zo + CW], 0.0, 2.0, AL.max, AL.mult, CW, 0.5, [zk], [ak])
+        else:
+            sact(T.ab[:, ao:ao + CW], T.zb[:, zo:zo + CW], AF.Abs, CW, [zk], [ak])
+        return zo, zk, ao, ak
+
+    def dist(v4, st, c, p, off, pen=None):
+        zo, zk, ao, ak = v4
+        two = (st, c) in RELU
+        if two:
+            mm([(off, off + LC, T.seln[:, q * 128:(q + 1) * 128], T.zb[:, zo + q:zo + CW:16], q == 0, False) for q in range(16)], CW, [zk, "seln"], p)
+        mm([(off, off + LC, T.selb[:, q * 128:(q + 1) * 128], T.ab[:, ao + q:ao + CW:16], q == 0 and not two, q == 15 and pen is None) for q in range(16)],
+           CW, [ak] + KSEL, p)
+        if pen is not None:
+            mm([(off, off + LC, T.idp[:, :], pen[0], False, True)], LC, pen[1] + ["idp"], p)
+
+    def home(t, c, L0, e0, LE, r1, xr, kxr, kdg):
+        L1, h, m = "L1_%d" % t, "g1_%d" % t, "m1_%d" % t
+        p = tile()
+        if c in SG1[t]:
+            go, gk = bufpair("gb", c)
+            add("s", GT_, lambda: g.scalar.activation(T.gb[:, go:go + CW], T.dcod[:, :].indirect(A(L0, c)), AF.Copy), ["code"] + K(L0, c), [gk])
+            diag(T.gb, gk, T.edb, KED, p, 0, go)
+            lk = "ln2_%d" % t
+            sact(A(lk, c), F(lambda: ps(p)[:, 0:LC]), AF.Ln, LC, (), K(lk, c), (p,))
+            vts(A(L1, c), A(lk, c), ALPHA, MID + 0.25, AL.mult, AL.add, LC, 1, K(lk, c), K(L1, c))
+        else:
+            add("v", GT_, lambda: g.vector.tensor_copy(T.gh[:, c * CW:(c + 1) * CW], T.dgs[:, :].indirect(A(L0, c))), kdg + K(L0, c), [("gh", c)])
+            diag(T.gh, ("gh", c), T.edh, ["edh"], p, 0, c * CW)
+            vcopy(A(L1, c), F(lambda: ps(p)[:, 0:LC]), LC, 1, (), K(L1, c), (p,))
+        yield
+        vcopy(A(h, c), A(L1, c), LC, 0.5, K(L1, c), K(h, c))
+        q = tile()
+        mm([(LC, 2 * LC, T.idh[:, :], A(e0, c), True, False), (LC, 2 * LC, T.idn[:, :], A(h, c), False, True)], 2 * LC, K(e0, c) + K(h, c) + ["idh", "idn"], q)
+        dist(view(T.xs, KX, A(L1, c), K(L1, c), xr, kxr, c, 1), 1, c, q, 0)
+        vts(A(r1, c), F(lambda: ps(q)[:, 0:LC]), T.pt[:, 0:1], None, AL.is_ge, None, LC, 1, ["pth"], K(r1, c), (q,))
+        vtt(A(m, c), A(r1, c), F(lambda: ps(q)[:, LC:2 * LC]), AL.mult, LC, 1, K(r1, c), K(m, c), (q,))
+        u = tile()
+        mm([(0, LC, T.idh[:, :], A(h, c), True, False), (0, LC, T.idh[:, :], A(m, c), False, True)], 2 * LC, K(h, c) + K(m, c) + ["idh"], u)
+        vcopy(A(LE, c), F(lambda: ps(u)[:, 0:LC]), LC, 1, (), K(LE, c), (u,))
+        yield
+
+    def walk(t, c, LE, r1, tb, xr, kxr):
+        X, kx, code, kc, th, kth = tb["X"], tb["kx"], tb["code"], tb["kc"], tb["th"], tb["kth"]
+        h1 = "h1_%d" % t
+        vcopy(A(h1, c), A(LE, c), LC, 0.5, K(LE, c), K(h1, c))
+        lst, hp, rp, ms = LE, h1, r1, []
+        for k in (2, 3, 4):
+            Lk, hk, lk, rk, mk = ["%s%d_%d" % (n, k, t) for n in ("L", "h", "ln", "r", "m")]
+            go, gk = bufpair("gb", c)
+
+            def gat(go=go, lst=lst):
+                return g.scalar.activation(T.gb[:, go:go + CW], code[:, :].indirect(A(lst, c)), AF.Copy)
+            add("s", GT_, gat, [kc] + K(lst, c), [gk])
+            p = tile()
+            diag(T.gb, gk, T.edb, KED, p, 0, go)
+            sact(A(lk, c), F(lambda p=p: ps(p)[:, 0:LC]), AF.Ln, LC, (), K(lk, c), (p,))
+            vts(A(Lk, c), A(lk, c), ALPHA, MID + 0.25, AL.mult, AL.add, LC, 1, K(lk, c), K(Lk, c))
+            vcopy(A(hk, c), A(Lk, c), LC, 0.5, K(Lk, c), K(hk, c))
+            q = tile()
+            mm([(LC, 2 * LC, T.idh[:, :], A(hp, c), True, False), (LC, 2 * LC, T.idn[:, :], A(hk, c), False, True)], 2 * LC,
+               K(hp, c) + K(hk, c) + ["idh", "idn"], q)
+            dist(view(X, kx, A(Lk, c), K(Lk, c), xr, kxr, c, k), k, c, q, 0, (A(rp, c), K(rp, c)))
+            vts(A(rk, c), F(lambda q=q: ps(q)[:, 0:LC]), th, None, AL.is_ge, None, LC, 1, [kth], K(rk, c), (q,))
+            vtt(A(mk, c), A(rk, c), F(lambda q=q: ps(q)[:, LC:2 * LC]), AL.mult, LC, 1, K(rk, c), K(mk, c), (q,))
+            lst, hp, rp = Lk, hk, rk
+            ms.append(mk)
+            yield
+        LF, hF = "LF_%d" % t, "hF_%d" % t
+        p = tile()
+        seq = [hp] + ms
+        mm([(0, LC, T.idh[:, :], A(x, c), i == 0, i == 3) for i, x in enumerate(seq)], 4 * LC, sum([K(x, c) for x in seq], []) + ["idh"], p)
+        vcopy(A(LF, c), F(lambda: ps(p)[:, 0:LC]), LC, 1, (), K(LF, c), (p,))
+        zo, zk, ao, ak = v4 = view(X, kx, A(LF, c), K(LF, c), xr, kxr, c, 5)
+        vcopy(A(hF, c), A(LF, c), LC, 0.5, K(LF, c), K(hF, c))
+        p2 = tile()
+        diag(T.zb, zk, T.edb, KED, p2, LC, zo)
+        bs, sq, ch, dS = "bs_%d" % t, "sq_%d" % t, "ch_%d" % t, "dS_%d" % t
+        sact(A(bs, c), F(lambda: ps(p2)[:, LC:2 * LC]), AF.Sign, LC, (), K(bs, c), (p2,), bias=-0.5)
+        p3 = tile()
+        dist(v4, 5, c, p3, 0)
+        sact(A(dS, c), F(lambda: ps(p3)[:, 0:LC]), AF.Copy, LC, (), K(dS, c), (p3,))
+        p4 = tile()
+        mm([(0, LC, tb["GT"], A(bs, c), True, True)], LC, K(bs, c) + [tb["kgt"]], p4)
+        sact(A(sq, c), F(lambda: ps(p4)[:, 0:LC]), AF.Square, LC, (), K(sq, c), (p4,))
+        p5 = tile()
+        mm([(0, LC, tb["aG"], A(sq, c), True, True), (LC, 2 * LC, T.blk[:, :], A(sq, c), True, True)], 2 * LC, K(sq, c) + [tb["kag"], "blk"], p5)
+        vts(A(ch, c), F(lambda: ps(p5)[:, 0:LC]), tb["nt"], None, AL.is_gt, None, LC, 1, [tb["knt"]], K(ch, c), (p5,))
+        sact(A("any", c), F(lambda: ps(p5)[:, LC:2 * LC]), AF.Sign, LC, (), K("any", c) + [("asum", t, c)], (p5,), bias=-16.0,
+             acc=T.asum[:, 4 * t + c:4 * t + c + 1])
+        yield
+
+    def keep(t, h, D0h):
+        c = -1 - h
+        dS, ch, hF, go = "dS_%d" % t, "ch_%d" % t, "hF_%d" % t, "go_%d" % t
+        p = tile()
+        mm([(0, 256, A(dS, c), T.dupf[:, :], True, False), (0, 256, T.onb[:, 0:128], T.prow[:, :], False, False)],
+           1024 + 256, K(dS, c) + ["dupf", "onb", "prow"], p)
+        mm([(0, 256, A(ch, c), T.dupb[:, :], False, True)], 256, K(ch, c) + ["dupb"], p)
+        add("v", vt(256, 1), lambda: g.vector.tensor_tensor_scan(T.pm[:, 256 * h:256 * h + 256], T.rst[:, :], ps(p)[:, 0:256], 0.0, AL.add, AL.min),
+            ["rst"], [("pm", h)], (p,))
+        for x in range(8):
+            vtt(T.eq[:, 128 * h + 16 * x:128 * h + 16 * x + 16], T.pm[:, 256 * h + 32 * x + 16:256 * h + 32 * x + 32],
+                F(lambda x=x: ps(p)[:, 32 * x + 16:32 * x + 32]), AL.is_equal, 16, 1, [("pm", h)], [("eq", h, x)], (p,))
+        q = tile()
+        mm([(0, 128, T.id37[:, :], A(hF, c), True, False), (0, 128, T.idn[:, :], A(D0h, c), False, False), (0, 128, T.idf[:, :], A(dS, c), False, True)],
+           768, K(hF, c) + K(D0h, c) + K(dS, c) + ["id37", "idn", "idf"], q)
+        u = tile()
+        mm([(0, 128, T.eq[:, 128 * h:128 * h + 128], T.idb[:, :], True, True)], 128, [("eq", h, x) for x in range(8)] + ["idb"], u)
+        vtt(A(go, c), A(ch, c), F(lambda: ps(u)[:, 0:128]), AL.is_gt, 128, 1, K(ch, c), K(go, c), (u,))
+        return q
+
+    def finish(t, out, D0f, wt):
+        p = tile()
+        mm([(0, 1, T.on16[:, :], T.asum[:, 4 * t + c:4 * t + c + 1], c == 0, c == NCH - 1) for c in range(NCH)], 4 * 4 * 64,
+           [("asum", t, c) for c in range(NCH)] + ["on16"], p)
+        vcopy(T.acol[:, t:t + 1], F(lambda: ps(p)[:, 0:1]), 1, 1, (), [("acol", t)], (p,))
+        go = "go_%d" % t
+        for c in (-1, -2):
+            vts(A("ga", c), F(lambda c=c: ps(wt[-1 - c])[:, 0:128]), T.acol[:, t:t + 1], None, AL.add, None, 128, 1, [("acol", t)], K("ga", c), (wt[-1 - c],))
+            vtt(A("mq", c), A(go, c), A("ga", c), AL.mult, 128, 2, K(go, c) + K("ga", c), K("mq", c))
+            vtt(A("qi", c), A("mq", c), A(D0f, c), AL.add, 128, 2, K("mq", c) + K(D0f, c), K("qi", c))
+            vts(A("ni", c), A("qi", c), W - 1, None, AL.bitwise_and, None, 128, 1, K("qi", c), K("ni", c))
+            vcopy(A(out, c), A("ni", c), 128, 1, K("ni", c), K(out, c))
+
+    def run(gens):
+        gens = list(enumerate(gens))
+        while gens:
+            nxt = []
+            for c, x in gens:
+                cur[0] = c
+                try:
+                    next(x)
+                    nxt.append((c, x))
+                except StopIteration:
+                    pass
+            gens = nxt
+        cur[0] = 0
+
+    vcopy(T.dgf[:, :], T.dgs[:, :], W, 1, [KDG], ["dgf"])
+    sact(T.dcod[:, :], T.dgf[:, :], AF.Exp, W, ["dgf"], ["code"], bias=-MID / ALPHA, scale=1.0 / ALPHA)
+
+    run(home(0, c, "L0a", "e0a", "LEa", "r1a", T.xr0, xr0k, [KDG]) for c in range(NCH))
+    last = None
+    for c in range(NCH):
+        last = send([s1, s1], [A("LEa", c), A("r1a", c)], [A("LEi", c), A("r1i", c)], ["re%d" % c, "re%d" % c], 1.0, K("LEa", c) + K("r1a", c),
+                    () if last is None else (last,))
+        recv("re%d" % c, 8, HOP, last, K("LEi", c) + K("r1i", c))
+
+    for k in range(3):
+        vts(T.gq[:, 128 * k:128 * k + 128], T.iq[:, :], T.tif[:, k:k + 1], T.sgf[:, k:k + 1], AL.is_equal, AL.mult, 128, 1, ["iq", "tif", "sgf"], [("gq", k)])
+    vtt(T.gq[:, 384:512], T.gq[:, 0:128], T.gq[:, 128:256], AL.add, 128, 2, [("gq", 0), ("gq", 1)], [("gq", 3)])
+    vtt(T.gq[:, 0:128], T.gq[:, 384:512], T.gq[:, 256:384], AL.add, 128, 2, [("gq", 3), ("gq", 2)], [("gq", 0)])
+    vtt(T.gj[:, :], T.gq[:, 0:128], T.blk[:, :], AL.mult, 128, 2, [("gq", 0), "blk"], ["gj"])
+    sact(T.pk[:, 128:256], T.gj[:, :], AF.Abs, 128, ["gj"], ["pkA"])
+    p0 = tile()
+    mm([(0, 128, T.gj[:, :], T.idb[:, :], True, True), (128, 129, T.pk[:, 128:256], T.onb[:, 0:1], True, True)], 192, ["gj", "idb", "pkA", "onb"], p0)
+    sact(T.pk[:, 0:128], F(lambda: ps(p0)[:, 0:128]), AF.Copy, 128, (), ["pkG"], (p0,))
+    vcopy(T.pt[:, 1:2], F(lambda: ps(p0)[:, 128:129]), 1, 1, (), ["ptn"], (p0,))
+    xrnk = xrep("xrn", A("xi"), K("xi"), "ssv")
+    vcopy(A("d0i"), A("L0i"), L, 0.5, K("L0i"), K("d0i"))
+    vcopy(A("d0f"), A("L0i"), L, 1, K("L0i"), K("d0f"))
+
+    h2 = dest(rank - 2)
+    k = send([h2, h2], [T.xs[:, :], T.dcod[:, :]], [T.xs2[:, :], T.code2[:, :]], ["rtab", "rtab"], 1.0, [KX, "code"], (last,), "ltab")
+    add("n", 0.0, None, ["code"], (), (), "ltab", 8, 25.0, [k])
+    recv("rtab", 8, 25.0, k, ["xs2", "code2"])
+    k = send([h2], [T.pk[:, :]], [T.pk2[:, :]], ["rpk"], 1.0, ["pkA", "pkG"], (k,))
+    recv("rpk", 8, 25.0, k, ["pk2"])
+    k = send([h2], [T.pt[:, 0:2]], [T.pt2[:, 0:2]], ["rpt"], 1.0, ["pth", "ptn"], (k,))
+    recv("rpt", 8, 25.0, k, ["pt2"])
+
+    vcopy(T.idf[:, :], T.idb[:, :], 128, 1, ["idb"], ["idf"])
+    vts(T.dupb[:, :], T.dupf[:, :], -BIGP, None, AL.mult, None, 256, 1, ["dupf"], ["dupb"])
+    vts(T.prow[:, :], T.iop[:, :], 1.0 / 4096, None, AL.mult, None, 256, 1, ["iop"], ["prow"])
+    add("v", vt(256, 1), lambda: g.vector.memset(T.rst[:, :], 0.0), (), ["rst"])
+    add("v", vt(8, 1), lambda: g.vector.memset(T.rst[:, 0:256:32], 2 * BIGP), (), ["rst"])
+    add("v", vt(128, 1), lambda: g.vector.memset(T.on16[:, :], 1.0 / 16), (), ["on16"])
+
+    tb = {"X": T.xs, "kx": KX, "code": T.dcod, "kc": "code", "th": T.pt[:, 0:1], "kth": "pth", "nt": T.pt[:, 1:2], "knt": "ptn",
+          "GT": T.pk[:, 0:128], "kgt": "pkG", "aG": T.pk[:, 128:256], "kag": "pkA"}
+    run(walk(0, c, "LEi", "r1i", tb, T.xrn, xrnk) for c in range(NCH))
+    wt = [keep(0, h, "d0i") for h in (0, 1)]
+    finish(0, "ndo", "d0f", wt)
+    d1, d2 = dest(rank - 1), dest(rank - 3)
+    k = send([d1], [A("ndo")], [A("ndi")], ["rnh"], 1.0, K("ndo"))
+    recv("rnh", 8, HOP, k, K("ndi"))
+    k = send([d2], [A("ndo")], [A("nd2")], ["rn2"], 1.0, K("ndo"), (k,))
+    recv("rn2", 8, HOP, k, K("nd2"))
+
+    vcopy(A("L0b"), T.dgs[:, 1:W:S], 256, 1, [KDG], K("L0b"))
+    vcopy(A("e0b"), A("L0b"), 256, 0.5, K("L0b"), K("e0b"))
+    xr1k = xrep("xr1", T.xs[:, 1:W:S], [KX], "vs")
+    if SG1[1]:
+        vcopy(A("ndg"), A("ndi"), 256, 1, K("ndi"), K("ndg"))
+        sact(T.dcod[:, 0:W:S], A("ndg"), AF.Exp, 256, K("ndg"), ["code"], bias=-MID / ALPHA, scale=1.0 / ALPHA)
+    vcopy(T.dgs[:, 0:W:S], A("ndi"), 256, 1, K("ndi"), [KDG])
+    run(home(1, c, "L0b", "e0b", "LEb", "r1b", T.xr1, xr1k, [KDG]) for c in range(NCH))
+    vcopy(A("ndf"), A("nd2"), 256, 1, K("nd2"), K("ndf"))
+    sact(T.code2[:, 0:W:S], A("ndf"), AF.Exp, 256, K("ndf"), ["code2"], bias=-MID / ALPHA, scale=1.0 / ALPHA)
+    vcopy(A("yd0"), A("ndi"), 256, 1, K("ndi"), K("yd0"))
+    add("y", 0.1, lambda: g.sync.dma_start(T.yd[:, 0:L], A("yd0")), K("yd0"), (), (), "ld5", 16, 2.0)
+    vcopy(A("d0f"), A("L0b"), L, 1, K("L0b"), K("d0f"))
+    tb = {"X": T.xs2, "kx": "xs2", "code": T.code2, "kc": "code2", "th": T.pt2[:, 0:1], "kth": "pt2", "nt": T.pt2[:, 1:2], "knt": "pt2",
+          "GT": T.pk2[:, 0:128], "kgt": "pk2", "aG": T.pk2[:, 128:256], "kag": "pk2"}
+    run(walk(1, c, "LEb", "r1b", tb, T.xr1, xr1k) for c in range(NCH))
+    vcopy(A("yef"), A("LF_1"), L, 1, K("LF_1"), K("yef"))
+    add("y", 0.1, lambda: g.sync.dma_start(T.ye[:, :], A("yef")), K("yef"), (), (), "ld6", 16, 2.0)
+    wt = [keep(1, h, "e0b") for h in (0, 1)]
+    finish(1, "yd1", "d0f", wt)
+    add("y", 0.1, lambda: g.sync.dma_start(T.yd[:, L:2 * L], A("yd1")), K("yd1"), (), (), "ld7", 16, 2.0)
+
+    order = schedule(ops, tiles, bankof)
+    emit(g, T, ENG, CSEM, ops, order, cnt["l"])
+
+
+def F(fn):
+    return (fn,)
+
+
+PW = 0.01
+SKEW = 2.0
+BONUS = {}
+
+
+def kind(o):
+    n = o["n"]
+    return (o["e"], str(n[0] if isinstance(n, tuple) else n))
+
+
+SEML = 0.1
+
+
+def schedule(ops, tiles, bankof):
+    n = len(ops)
+    succ = [[] for _ in range(n)]
+    for k in range(n):
+        for d in ops[k]["deps"]:
+            succ[d].append(k)
+    bl = [0.0] * n
+    for k in range(n - 1, -1, -1):
+        o = ops[k]
+        bl[k] = o["d"] + o["lat"] + max([bl[s] for s in succ[k]] + [0.0])
+    tfirst = {}
+    for t, lst in enumerate(tiles):
+        if lst:
+            tfirst[lst[0]] = t
+    tleft = [len(x) for x in tiles]
+    bank = [None] * 8
+    bfree = [(0.0, None)] * 8
+    left = [len(o["deps"]) for o in ops]
+    ready = [k for k in range(n) if left[k] == 0]
+    fin = [0.0] * n
+    free = {}
+    order = []
+    while ready:
+        best = None
+        for k in ready:
+            o = ops[k]
+            st = free.get(o["e"], 0.0) if o["e"] != "n" else 0.0
+            for d in o["deps"]:
+                x = fin[d] + (SEML if ops[d]["e"] != o["e"] else 0.05)
+                if x > st:
+                    st = x
+            b = -1
+            if k in tfirst:
+                cand = [(bfree[i][0], i) for i in range(8) if bank[i] is None]
+                if not cand:
+                    continue
+                f, b = min(cand)
+                st = max(st, f + SEML if f > 0 else 0.0)
+            key = (st - PW * (bl[k] - SKEW * o["c"] + BONUS.get(kind(o), 0.0)), k)
+            if best is None or key < best[0]:
+                best = (key, k, st, b)
+        if best is None:
+            raise ValueError("no free PSUM bank")
+        _, k, st, b = best
+        o = ops[k]
+        ready.remove(k)
+        if b >= 0:
+            t = tfirst[k]
+            bankof[t] = b
+            bank[b] = t
+            if bfree[b][1] is not None:
+                o["deps"].add(bfree[b][1])
+        if o["e"] != "n":
+            free[o["e"]] = st + o["d"]
+        fin[k] = st + o["d"] + o["lat"]
+        o["st"] = st
+        order.append(k)
+        for t in o["ps"]:
+            tleft[t] -= 1
+            if tleft[t] == 0:
+                bb = bankof[t]
+                bank[bb] = None
+                bfree[bb] = (fin[k], k)
+        for s in succ[k]:
+            left[s] -= 1
+            if left[s] == 0:
+                ready.append(s)
+    return order
+
+
+def emit(g, T, ENG, CSEM, ops, order, nlocal):
+    count = {"v": 0, "s": 0, "p": 0, "g": 0}
+    known = {e: {} for e in ENG}
+    done = {}
+    waited = {}
+    for k in order:
+        o = ops[k]
+        e = o["e"]
+        if e == "n":
+            done[k] = (o["sem"], o["inc"], {})
+            continue
+        q = ENG[e]
+        need = {}
+        imp = dict(known[e])
+        for d in o["deps"]:
+            if done[d] is None or d in o["soft"]:
+                continue
+            if e == "p" and ops[d]["e"] == "p":
+                continue
+            s, v, _i = done[d]
+            if known[e].get(s, 0) < v and need.get(s, (0, 0))[0] < v:
+                need[s] = (v, d)
+        for s in list(need):
+            v, d = need[s]
+            for s2 in need:
+                if s2 != s and done[need[s2][1]][2].get(s, 0) >= v:
+                    del need[s]
+                    break
+        for s in need:
+            v, d = need[s]
+            q.wait_ge(T.sem[s], v)
+            waited[s] = max(waited.get(s, 0), v)
+            for a, b in done[d][2].items():
+                if known[e].get(a, 0) < b:
+                    known[e][a] = b
+            known[e][s] = max(known[e].get(s, 0), v)
+        inst = o["f"]()
+        if o["sem"] == "-":
+            done[k] = None
+            continue
+        if o["sem"] is None:
+            count[e] += 1
+            s, v = CSEM[e], count[e]
+            inst.then_inc(T.sem[s], 1)
+        else:
+            s, v = o["sem"], o["inc"]
+            inst.then_inc(T.sem[s], v)
+        done[k] = (s, v, dict(known[e]))
+    total = {CSEM[e]: count[e] for e in count if count[e]}
+    total["lsem"] = nlocal
+    for k in order:
+        o = ops[k]
+        if o["sem"] not in (None, "-"):
+            total[o["sem"]] = o["inc"]
+    for s in total:
+        if waited.get(s, 0) < total[s]:
+            g.wait_ge(T.sem[s], total[s])

@@ -12,7 +12,7 @@ AL = AluOpType
 AF = ActivationFunctionType
 
 U_ = ["L0a", "L0b", "L0i", "LEa", "LEb", "LEi", "L1_0", "L1_1", "ndo", "ndi", "nd2"] + ["%s_%d" % (n, t) for n in ("L2", "L3", "L4", "LF") for t in (0, 1)]
-H_ = ["e0a", "e0b", "d0i"] + ["%s_%d" % (n, t) for n in ("h1", "m1", "g1", "h2", "h3", "h4", "hF", "m2", "m3", "m4") for t in (0, 1)]
+H_ = ["e0b", "d0i", "wd", "mh"] + ["%s_%d" % (n, t) for n in ("h1", "m1", "g1", "h2", "h3", "h4", "hF", "m2", "m3", "m4") for t in (0, 1)]
 F_ = ["d0f", "dS_0", "dS_1", "mq", "q", "ga", "yd0", "yd1", "yef", "ndf", "ndg"] + ["ln%d_%d" % (k, t) for k in (2, 3, 4) for t in (0, 1)]
 B_ = ["x0", "xi", "r1a", "r1b", "r1i", "any"] + ["%s_%d" % (n, t) for n in ("r2", "r3", "r4", "bs", "sq", "ch", "go") for t in (0, 1)]
 I_ = ["qi", "ni"]
@@ -32,8 +32,8 @@ SCRATCH.update({
     "gh": ("sbuf", [128, 16 * L], "float16"),
     "selb": ("sbuf", [128, 2048], "bfloat16"), "seln": ("sbuf", [128, 2048], "bfloat16"), "edb": ("sbuf", [128, 2048], "bfloat16"), "edh": ("sbuf", [128, 2048], "float16"),
     "onb": ("sbuf", [128, 256], "bfloat16"), "onf": ("sbuf", [128, 256], "float32"), "on16": ("sbuf", [128, 128], "float32"),
-    "idb": ("sbuf", [128, 128], "bfloat16"), "idh": ("sbuf", [128, 128], "float16"), "idn": ("sbuf", [128, 128], "float16"),
-    "id37": ("sbuf", [128, 128], "float16"), "idp": ("sbuf", [128, 128], "bfloat16"), "idf": ("sbuf", [128, 128], "float32"),
+    "idb": ("sbuf", [128, 128], "bfloat16"), "idh": ("sbuf", [128, 128], "float16"), "idn": ("sbuf", [128, 128], "float16"), "idq": ("sbuf", [128, 128], "float16"), "idm": ("sbuf", [128, 128], "float16"),
+    "id37": ("sbuf", [128, 128], "float16"), "idp": ("sbuf", [128, 128], "bfloat16"), "idnb": ("sbuf", [128, 128], "bfloat16"), "idf": ("sbuf", [128, 128], "float32"),
     "blk0": ("sbuf", [128, 128], "bfloat16"), "blk": ("sbuf", [128, 128], "bfloat16"),
     "dupf": ("sbuf", [128, 256], "float32"), "dupb": ("sbuf", [128, 256], "bfloat16"), "iop": ("sbuf", [128, 256], "float32"),
     "prow": ("sbuf", [128, 256], "bfloat16"), "rst": ("sbuf", [128, 256], "float32"),
@@ -42,16 +42,19 @@ SCRATCH.update({
     "tif": ("sbuf", [128, 4], "float32"), "sgf": ("sbuf", [128, 4], "float32"),
     "gq": ("sbuf", [128, 512], "float32"), "gj": ("sbuf", [128, 128], "bfloat16"),
     "pk": ("sbuf", [128, 256], "bfloat16"), "pk2": ("sbuf", [128, 256], "bfloat16"),
-    "pt": ("sbuf", [128, 4], "float32"), "pt2": ("sbuf", [128, 4], "float32"),
+    "pt": ("sbuf", [128, 8], "float32"), "pt2": ("sbuf", [128, 8], "float32"),
     "asum": ("sbuf", [128, 8], "float32"), "acol": ("sbuf", [128, 8], "float32"),
 })
 for _k in range(8):
     SCRATCH["bank%d" % _k] = ("psum", [128, 512], "float32")
-SEMAPHORES = ["cv", "cs", "cp", "cg", "lsem", "ltab", "rx", "rtab", "rpk", "rpt", "rnh", "rn2"] + ["re%d" % c for c in range(NCH)] + ["ld%d" % k for k in range(10)]
+SEMAPHORES = ["cv", "cs", "cp", "cg", "lsem", "ltab", "rx", "rtab", "rpk", "rpt", "rnh", "rn2"] + ["re%d" % c for c in range(NCH)] + ["rr%d" % c for c in range(NCH)] + ["ld%d" % k for k in range(10)]
 
 CY = 0.83e-3 * 1.2
-RELU = {(1, 0), (1, 1), (5, 3)}
-SG1 = ((1, 2, 3), (1, 2, 3))
+RELU = {(1, 0), (1, 2), (2, 3), (3, 3)}
+SG1 = ((1, 2), (0, 1))
+RS = ()
+CHS = True
+EDV, XR0, XRN, XR1 = "ssvsssssssvsssvs", "ssv", "v", "vs"
 GC = 1.5
 HOP = 2.5
 
@@ -166,12 +169,13 @@ def rank_program(g, core, T, topo):
         q = g.sync if eng == "y" else g.scalar
         return add(eng, 0.1, lambda: q.dma_start(buf, src), (), [(sem, "ld")], (), sem, 16, lat)
 
-    load("y", T.dgs[:, :], T.dg[:, :], "ld1", 7.0)
+    load("y", T.dgs[:, 0:W // 2], T.dg[:, 0:W // 2], "ld1", 4.5)
+    load("y", T.dgs[:, W // 2:W], T.dg[:, W // 2:W], "ld8", 7.0)
     load("y", T.xs[:, :], T.xv[:, :], "ld0", 9.0)
     load("y", T.thi[:, 0:1], T.th[:, :], "ld4", 9.5)
     load("y", T.tii[:, 0:3], T.ti[:, :], "ld2", 9.5)
     load("y", T.sgi[:, 0:3], T.sg[:, :], "ld3", 9.5)
-    KX, KDG = ("ld0", "ld"), ("ld1", "ld")
+    KX, KDG = ("ld0", "ld"), [("ld1", "ld"), ("ld8", "ld")]
 
     add("v", vt(256, 0.5), lambda: g.vector.memset(T.onb[:, :], 1.0), (), ["onb"])
     add("v", vt(256, 1), lambda: g.vector.memset(T.onf[:, :], 1.0), (), ["onf"])
@@ -185,8 +189,10 @@ def rank_program(g, core, T, topo):
     add("g", 0.6, lambda: g.iota(T.iop[:, :], [[0, 8], [0, 2], [1, 16]], 0, 0, allow_small_or_imprecise_dtypes=True), (), ["iop"])
     for p in range(16):
         def cp(p=p):
-            return g.vector.tensor_copy(T.edb[:, p * 128 + p:(p + 1) * 128:16], T.idb[:, p:128:16])
-        add("v", vt(8, 1), cp, ["idb", "edb0"], [("edb", p)])
+            if EDV[p] == "v":
+                return g.vector.tensor_copy(T.edb[:, p * 128 + p:(p + 1) * 128:16], T.idb[:, p:128:16])
+            return g.scalar.activation(T.edb[:, p * 128 + p:(p + 1) * 128:16], T.idb[:, p:128:16], AF.Copy)
+        add(EDV[p], vt(8, 1), cp, ["idb", "edb0"], [("edb", p)])
     KED = [("edb", p) for p in range(16)]
     vcopy(T.edh[:, :], T.edb[:, :], 2048, 0.5, KED, ["edh"])
     for p in range(16):
@@ -199,7 +205,9 @@ def rank_program(g, core, T, topo):
     vcopy(T.idh[:, :], T.idb[:, :], 128, 0.5, ["idb"], ["idh"])
     vts(T.idn[:, :], T.idb[:, :], -1.0, None, AL.mult, None, 128, 0.5, ["idb"], ["idn"])
     vts(T.id37[:, :], T.idb[:, :], 37.0, None, AL.mult, None, 128, 0.5, ["idb"], ["id37"])
-    vts(T.idp[:, :], T.idb[:, :], BIGP, None, AL.mult, None, 128, 0.5, ["idb"], ["idp"])
+    vts(T.idp[:, :], T.idb[:, :], BIGP / 2, None, AL.mult, None, 128, 0.5, ["idb"], ["idp"])
+    vts(T.idq[:, :], T.idb[:, :], 0.5, None, AL.mult, None, 128, 0.5, ["idb"], ["idq"])
+    vts(T.idm[:, :], T.idb[:, :], -0.5, None, AL.mult, None, 128, 0.5, ["idb"], ["idm"])
 
     def xrep(buf, src, rk, engs):
         keys = []
@@ -214,14 +222,16 @@ def rank_program(g, core, T, topo):
                 sact(o, src, AF.Copy, 256, rk, [key])
         return keys
 
-    xr0k = xrep("xr0", T.xs[:, 0:W:S], [KX], "vs")
+    xr0k = xrep("xr0", T.xs[:, 0:W:S], [KX], XR0)
     vcopy(A("x0"), T.xs[:, 0:W:S], 256, 0.5, [KX], K("x0"))
-    vcopy(A("L0a"), T.dgs[:, 0:W:S], 256, 1, [KDG], K("L0a"))
-    vcopy(A("e0a"), A("L0a"), 256, 0.5, K("L0a"), K("e0a"))
+    for h in (0, 1):
+        vcopy(A("L0a", -1 - h), T.dgs[:, h * W // 2:(h + 1) * W // 2:S], 128, 1, [KDG[h]], K("L0a", -1 - h))
 
     vcopy(T.tif[:, 0:3], T.tii[:, 0:3], 3, 1, [("ld2", "ld")], ["tif"])
     vcopy(T.sgf[:, 0:3], T.sgi[:, 0:3], 3, 1, [("ld3", "ld")], ["sgf"])
-    vcopy(T.pt[:, 0:1], T.thi[:, 0:1], 1, 1, [("ld4", "ld")], ["pth"])
+    for j, (a, b) in enumerate(((-1.0, 0.5), (-1.0, 0.5 + BIGP / 2), (1.0, 0.0), (1.0, -BIGP / 2))):
+        vts(T.pt[:, j:j + 1], T.thi[:, 0:1], a, b, AL.mult, AL.add, 1, 1, [("ld4", "ld")], ["ptk"])
+    PTK = ["ptk"]
 
     def dest(r):
         return cores[r % N]
@@ -290,8 +300,14 @@ def rank_program(g, core, T, topo):
         if pen is not None:
             mm([(off, off + LC, T.idp[:, :], pen[0], False, True)], LC, pen[1] + ["idp"], p)
 
-    def home(t, c, L0, e0, LE, r1, xr, kxr, kdg):
-        L1, h, m = "L1_%d" % t, "g1_%d" % t, "m1_%d" % t
+    def rest(k, c, rk, q, th, kth):
+        j = 1 if (k - 1) in RS else 0
+        if k in RS:
+            sact(A(rk, c), F(lambda: ps(q)[:, 0:LC]), AF.Sign, LC, [kth], K(rk, c), (q,), bias=th[:, j:j + 1])
+        else:
+            vts(A(rk, c), F(lambda: ps(q)[:, 0:LC]), th[:, 2 + j:3 + j], 2.0, AL.is_ge, AL.mult, LC, 1, [kth], K(rk, c), (q,))
+
+    def home(t, c, L0, L1, r1, xr, kxr, kdg):
         p = tile()
         if c in SG1[t]:
             go, gk = bufpair("gb", c)
@@ -305,22 +321,17 @@ def rank_program(g, core, T, topo):
             diag(T.gh, ("gh", c), T.edh, ["edh"], p, 0, c * CW)
             vcopy(A(L1, c), F(lambda: ps(p)[:, 0:LC]), LC, 1, (), K(L1, c), (p,))
         yield
-        vcopy(A(h, c), A(L1, c), LC, 0.5, K(L1, c), K(h, c))
         q = tile()
-        mm([(LC, 2 * LC, T.idh[:, :], A(e0, c), True, False), (LC, 2 * LC, T.idn[:, :], A(h, c), False, True)], 2 * LC, K(e0, c) + K(h, c) + ["idh", "idn"], q)
         dist(view(T.xs, KX, A(L1, c), K(L1, c), xr, kxr, c, 1), 1, c, q, 0)
-        vts(A(r1, c), F(lambda: ps(q)[:, 0:LC]), T.pt[:, 0:1], None, AL.is_ge, None, LC, 1, ["pth"], K(r1, c), (q,))
-        vtt(A(m, c), A(r1, c), F(lambda: ps(q)[:, LC:2 * LC]), AL.mult, LC, 1, K(r1, c), K(m, c), (q,))
-        u = tile()
-        mm([(0, LC, T.idh[:, :], A(h, c), True, False), (0, LC, T.idh[:, :], A(m, c), False, True)], 2 * LC, K(h, c) + K(m, c) + ["idh"], u)
-        vcopy(A(LE, c), F(lambda: ps(u)[:, 0:LC]), LC, 1, (), K(LE, c), (u,))
+        rest(1, c, r1, q, T.pt, "ptk")
         yield
 
-    def walk(t, c, LE, r1, tb, xr, kxr):
+    def walk(t, c, L1, r1, e0, tb, xr, kxr):
         X, kx, code, kc, th, kth = tb["X"], tb["kx"], tb["code"], tb["kc"], tb["th"], tb["kth"]
         h1 = "h1_%d" % t
-        vcopy(A(h1, c), A(LE, c), LC, 0.5, K(LE, c), K(h1, c))
-        lst, hp, rp, ms = LE, h1, r1, []
+        m1 = "m1_%d" % t
+        vcopy(A(h1, c), A(L1, c), LC, 0.5, K(L1, c), K(h1, c))
+        lst, hp, rp, ms = L1, h1, r1, [m1]
         for k in (2, 3, 4):
             Lk, hk, lk, rk, mk = ["%s%d_%d" % (n, k, t) for n in ("L", "h", "ln", "r", "m")]
             go, gk = bufpair("gb", c)
@@ -336,16 +347,24 @@ def rank_program(g, core, T, topo):
             q = tile()
             mm([(LC, 2 * LC, T.idh[:, :], A(hp, c), True, False), (LC, 2 * LC, T.idn[:, :], A(hk, c), False, True)], 2 * LC,
                K(hp, c) + K(hk, c) + ["idh", "idn"], q)
+            if k == 2:
+                mm([(2 * LC, 3 * LC, T.idh[:, :], A(e0, c), True, False), (2 * LC, 3 * LC, T.idn[:, :], A(h1, c), False, True)], 2 * LC,
+                   K(e0, c) + K(h1, c) + ["idh", "idn"], q)
+                vtt(A(m1, c), A(r1, c), F(lambda q=q: ps(q)[:, 2 * LC:3 * LC]), AL.mult, LC, 1, K(r1, c), K(m1, c), (q,))
             dist(view(X, kx, A(Lk, c), K(Lk, c), xr, kxr, c, k), k, c, q, 0, (A(rp, c), K(rp, c)))
-            vts(A(rk, c), F(lambda q=q: ps(q)[:, 0:LC]), th, None, AL.is_ge, None, LC, 1, [kth], K(rk, c), (q,))
+            rest(k, c, rk, q, th, kth)
             vtt(A(mk, c), A(rk, c), F(lambda q=q: ps(q)[:, LC:2 * LC]), AL.mult, LC, 1, K(rk, c), K(mk, c), (q,))
             lst, hp, rp = Lk, hk, rk
             ms.append(mk)
             yield
         LF, hF = "LF_%d" % t, "hF_%d" % t
         p = tile()
-        seq = [hp] + ms
-        mm([(0, LC, T.idh[:, :], A(x, c), i == 0, i == 3) for i, x in enumerate(seq)], 4 * LC, sum([K(x, c) for x in seq], []) + ["idh"], p)
+        hs = [e0, h1] + ["h%d_%d" % (k, t) for k in (2, 3, 4)]
+        seq = [(T.idh, hp)] + [(T.idq, x) for x in ms]
+        for k in RS:
+            seq += [(T.idq, hs[k - 1]), (T.idm, hs[k])]
+        mm([(0, LC, w[:, :], A(x, c), i == 0, i == len(seq) - 1) for i, (w, x) in enumerate(seq)], len(seq) * LC,
+           sum([K(x, c) for w, x in seq], []) + ["idq", "idh", "idm"], p)
         vcopy(A(LF, c), F(lambda: ps(p)[:, 0:LC]), LC, 1, (), K(LF, c), (p,))
         zo, zk, ao, ak = v4 = view(X, kx, A(LF, c), K(LF, c), xr, kxr, c, 5)
         vcopy(A(hF, c), A(LF, c), LC, 0.5, K(LF, c), K(hF, c))
@@ -361,7 +380,10 @@ def rank_program(g, core, T, topo):
         sact(A(sq, c), F(lambda: ps(p4)[:, 0:LC]), AF.Square, LC, (), K(sq, c), (p4,))
         p5 = tile()
         mm([(0, LC, tb["aG"], A(sq, c), True, True), (LC, 2 * LC, T.blk[:, :], A(sq, c), True, True)], 2 * LC, K(sq, c) + [tb["kag"], "blk"], p5)
-        vts(A(ch, c), F(lambda: ps(p5)[:, 0:LC]), tb["nt"], None, AL.is_gt, None, LC, 1, [tb["knt"]], K(ch, c), (p5,))
+        if CHS:
+            sact(A(ch, c), F(lambda: ps(p5)[:, 0:LC]), AF.Sign, LC, [tb["knt"]], K(ch, c), (p5,), bias=tb["nt"][:, 4:5])
+        else:
+            vts(A(ch, c), F(lambda: ps(p5)[:, 0:LC]), tb["nt"][:, 5:6], None, AL.is_gt, None, LC, 1, [tb["knt"]], K(ch, c), (p5,))
         sact(A("any", c), F(lambda: ps(p5)[:, LC:2 * LC]), AF.Sign, LC, (), K("any", c) + [("asum", t, c)], (p5,), bias=-16.0,
              acc=T.asum[:, 4 * t + c:4 * t + c + 1])
         yield
@@ -373,31 +395,33 @@ def rank_program(g, core, T, topo):
         mm([(0, 256, A(dS, c), T.dupf[:, :], True, False), (0, 256, T.onb[:, 0:128], T.prow[:, :], False, False)],
            1024 + 256, K(dS, c) + ["dupf", "onb", "prow"], p)
         mm([(0, 256, A(ch, c), T.dupb[:, :], False, True)], 256, K(ch, c) + ["dupb"], p)
-        add("v", vt(256, 1), lambda: g.vector.tensor_tensor_scan(T.pm[:, 256 * h:256 * h + 256], T.rst[:, :], ps(p)[:, 0:256], 0.0, AL.add, AL.min),
+        add("v", vt(256, 1), lambda: g.vector.tensor_tensor_scan(T.pm[:, 256 * h:256 * h + 256], T.rst[:, :], ps(p)[:, 0:256], 0.0, AL.mult, AL.min),
             ["rst"], [("pm", h)], (p,))
         for x in range(8):
             vtt(T.eq[:, 128 * h + 16 * x:128 * h + 16 * x + 16], T.pm[:, 256 * h + 32 * x + 16:256 * h + 32 * x + 32],
                 F(lambda x=x: ps(p)[:, 32 * x + 16:32 * x + 32]), AL.is_equal, 16, 1, [("pm", h)], [("eq", h, x)], (p,))
         q = tile()
-        mm([(0, 128, T.id37[:, :], A(hF, c), True, False), (0, 128, T.idn[:, :], A(D0h, c), False, False), (0, 128, T.idf[:, :], A(dS, c), False, True)],
-           768, K(hF, c) + K(D0h, c) + K(dS, c) + ["id37", "idn", "idf"], q)
+        mm([(0, 128, T.id37[:, :], A(hF, c), True, False), (0, 128, T.idf[:, :], A(dS, c), False, True)],
+           640, K(hF, c) + K(dS, c) + ["id37", "idf"], q)
         u = tile()
-        mm([(0, 128, T.eq[:, 128 * h:128 * h + 128], T.idb[:, :], True, True)], 128, [("eq", h, x) for x in range(8)] + ["idb"], u)
-        vtt(A(go, c), A(ch, c), F(lambda: ps(u)[:, 0:128]), AL.is_gt, 128, 1, K(ch, c), K(go, c), (u,))
-        return q
+        mm([(0, 128, T.idb[:, :], A(ch, c), True, False)], 128, K(ch, c) + ["idb"], u)
+        mm([(0, 128, T.eq[:, 128 * h:128 * h + 128], T.idnb[:, :], False, True)], 128, [("eq", h, x) for x in range(8)] + ["idnb"], u)
+        return q, u
 
-    def finish(t, out, D0f, wt):
+    def finish(t, out, D0f, D0h, wt):
         p = tile()
         mm([(0, 1, T.on16[:, :], T.asum[:, 4 * t + c:4 * t + c + 1], c == 0, c == NCH - 1) for c in range(NCH)], 4 * 4 * 64,
            [("asum", t, c) for c in range(NCH)] + ["on16"], p)
         vcopy(T.acol[:, t:t + 1], F(lambda: ps(p)[:, 0:1]), 1, 1, (), [("acol", t)], (p,))
-        go = "go_%d" % t
         for c in (-1, -2):
-            vts(A("ga", c), F(lambda c=c: ps(wt[-1 - c])[:, 0:128]), T.acol[:, t:t + 1], None, AL.add, None, 128, 1, [("acol", t)], K("ga", c), (wt[-1 - c],))
-            vtt(A("mq", c), A(go, c), A("ga", c), AL.mult, 128, 2, K(go, c) + K("ga", c), K("mq", c))
-            vtt(A("qi", c), A("mq", c), A(D0f, c), AL.add, 128, 2, K("mq", c) + K(D0f, c), K("qi", c))
+            q, u = wt[-1 - c]
+            vts(A("qi", c), F(lambda q=q: ps(q)[:, 0:128]), T.acol[:, t:t + 1], None, AL.add, None, 128, 1, [("acol", t)], K("qi", c), (q,))
             vts(A("ni", c), A("qi", c), W - 1, None, AL.bitwise_and, None, 128, 1, K("qi", c), K("ni", c))
-            vcopy(A(out, c), A("ni", c), 128, 1, K("ni", c), K(out, c))
+            vtt(A("wd", c), A("ni", c), A(D0f, c), AL.subtract, 128, 2, K("ni", c) + K(D0f, c), K("wd", c))
+            vtt(A("mh", c), A("wd", c), F(lambda u=u: ps(u)[:, 0:128]), AL.mult, 128, 1, K("wd", c), K("mh", c), (u,))
+            v = tile()
+            mm([(0, 128, T.idh[:, :], A(D0h, c), True, False), (0, 128, T.idh[:, :], A("mh", c), False, True)], 256, K(D0h, c) + K("mh", c) + ["idh"], v)
+            vcopy(A(out, c), F(lambda v=v: ps(v)[:, 0:128]), 128, 1, (), K(out, c), (v,))
 
     def run(gens):
         gens = list(enumerate(gens))
@@ -413,15 +437,18 @@ def rank_program(g, core, T, topo):
             gens = nxt
         cur[0] = 0
 
-    vcopy(T.dgf[:, :], T.dgs[:, :], W, 1, [KDG], ["dgf"])
-    sact(T.dcod[:, :], T.dgf[:, :], AF.Exp, W, ["dgf"], ["code"], bias=-MID / ALPHA, scale=1.0 / ALPHA)
+    for h in (0, 1):
+        a, b = h * W // 2, (h + 1) * W // 2
+        vcopy(T.dgf[:, a:b], T.dgs[:, a:b], W // 2, 1, [KDG[h]], [("dgf", h)])
+        sact(T.dcod[:, a:b], T.dgf[:, a:b], AF.Exp, W // 2, [("dgf", h)], ["code"], bias=-MID / ALPHA, scale=1.0 / ALPHA)
 
-    run(home(0, c, "L0a", "e0a", "LEa", "r1a", T.xr0, xr0k, [KDG]) for c in range(NCH))
-    last = None
+    run(home(0, c, "L0a", "LEa", "r1a", T.xr0, xr0k, KDG) for c in range(NCH))
     for c in range(NCH):
-        last = send([s1, s1], [A("LEa", c), A("r1a", c)], [A("LEi", c), A("r1i", c)], ["re%d" % c, "re%d" % c], 1.0, K("LEa", c) + K("r1a", c),
-                    () if last is None else (last,))
-        recv("re%d" % c, 8, HOP, last, K("LEi", c) + K("r1i", c))
+        last = send([s1], [A("LEa", c)], [A("LEi", c)], ["re%d" % c], 1.0, K("LEa", c))
+        recv("re%d" % c, 8, HOP, last, K("LEi", c))
+    for c in range(NCH):
+        last = send([s1], [A("r1a", c)], [A("r1i", c)], ["rr%d" % c], 1.0, K("r1a", c))
+        recv("rr%d" % c, 8, HOP, last, K("r1i", c))
 
     for k in range(3):
         vts(T.gq[:, 128 * k:128 * k + 128], T.iq[:, :], T.tif[:, k:k + 1], T.sgf[:, k:k + 1], AL.is_equal, AL.mult, 128, 1, ["iq", "tif", "sgf"], [("gq", k)])
@@ -432,8 +459,9 @@ def rank_program(g, core, T, topo):
     p0 = tile()
     mm([(0, 128, T.gj[:, :], T.idb[:, :], True, True), (128, 129, T.pk[:, 128:256], T.onb[:, 0:1], True, True)], 192, ["gj", "idb", "pkA", "onb"], p0)
     sact(T.pk[:, 0:128], F(lambda: ps(p0)[:, 0:128]), AF.Copy, 128, (), ["pkG"], (p0,))
-    vcopy(T.pt[:, 1:2], F(lambda: ps(p0)[:, 128:129]), 1, 1, (), ["ptn"], (p0,))
-    xrnk = xrep("xrn", A("xi"), K("xi"), "ssv")
+    vts(T.pt[:, 4:5], F(lambda: ps(p0)[:, 128:129]), -1.0, None, AL.mult, None, 1, 1, (), ["ptn"], (p0,))
+    vcopy(T.pt[:, 5:6], F(lambda: ps(p0)[:, 128:129]), 1, 1, (), ["ptn"], (p0,))
+    xrnk = xrep("xrn", A("xi"), K("xi"), XRN)
     vcopy(A("d0i"), A("L0i"), L, 0.5, K("L0i"), K("d0i"))
     vcopy(A("d0f"), A("L0i"), L, 1, K("L0i"), K("d0f"))
 
@@ -443,47 +471,48 @@ def rank_program(g, core, T, topo):
     recv("rtab", 8, 25.0, k, ["xs2", "code2"])
     k = send([h2], [T.pk[:, :]], [T.pk2[:, :]], ["rpk"], 1.0, ["pkA", "pkG"], (k,))
     recv("rpk", 8, 25.0, k, ["pk2"])
-    k = send([h2], [T.pt[:, 0:2]], [T.pt2[:, 0:2]], ["rpt"], 1.0, ["pth", "ptn"], (k,))
+    k = send([h2], [T.pt[:, 0:6]], [T.pt2[:, 0:6]], ["rpt"], 1.0, PTK + ["ptn"], (k,))
     recv("rpt", 8, 25.0, k, ["pt2"])
 
     vcopy(T.idf[:, :], T.idb[:, :], 128, 1, ["idb"], ["idf"])
     vts(T.dupb[:, :], T.dupf[:, :], -BIGP, None, AL.mult, None, 256, 1, ["dupf"], ["dupb"])
-    vts(T.prow[:, :], T.iop[:, :], 1.0 / 4096, None, AL.mult, None, 256, 1, ["iop"], ["prow"])
-    add("v", vt(256, 1), lambda: g.vector.memset(T.rst[:, :], 0.0), (), ["rst"])
-    add("v", vt(8, 1), lambda: g.vector.memset(T.rst[:, 0:256:32], 2 * BIGP), (), ["rst"])
+    vts(T.prow[:, :], T.iop[:, :], 1.0 / 4096, 1.0 / 8192, AL.mult, AL.add, 256, 1, ["iop"], ["prow"])
+    add("v", vt(256, 1), lambda: g.vector.memset(T.rst[:, :], 1.0), (), ["rst"])
+    add("v", vt(8, 1), lambda: g.vector.memset(T.rst[:, 0:256:32], 0.0), (), ["rst"])
+    vts(T.idnb[:, :], T.idb[:, :], -1.0, None, AL.mult, None, 128, 0.5, ["idb"], ["idnb"])
     add("v", vt(128, 1), lambda: g.vector.memset(T.on16[:, :], 1.0 / 16), (), ["on16"])
 
-    tb = {"X": T.xs, "kx": KX, "code": T.dcod, "kc": "code", "th": T.pt[:, 0:1], "kth": "pth", "nt": T.pt[:, 1:2], "knt": "ptn",
+    tb = {"X": T.xs, "kx": KX, "code": T.dcod, "kc": "code", "th": T.pt, "kth": "ptk", "nt": T.pt, "knt": "ptn",
           "GT": T.pk[:, 0:128], "kgt": "pkG", "aG": T.pk[:, 128:256], "kag": "pkA"}
-    run(walk(0, c, "LEi", "r1i", tb, T.xrn, xrnk) for c in range(NCH))
+    run(walk(0, c, "LEi", "r1i", "d0i", tb, T.xrn, xrnk) for c in range(NCH))
     wt = [keep(0, h, "d0i") for h in (0, 1)]
-    finish(0, "ndo", "d0f", wt)
+    finish(0, "ndo", "d0f", "d0i", wt)
     d1, d2 = dest(rank - 1), dest(rank - 3)
     k = send([d1], [A("ndo")], [A("ndi")], ["rnh"], 1.0, K("ndo"))
     recv("rnh", 8, HOP, k, K("ndi"))
     k = send([d2], [A("ndo")], [A("nd2")], ["rn2"], 1.0, K("ndo"), (k,))
     recv("rn2", 8, HOP, k, K("nd2"))
 
-    vcopy(A("L0b"), T.dgs[:, 1:W:S], 256, 1, [KDG], K("L0b"))
+    vcopy(A("L0b"), T.dgs[:, 1:W:S], 256, 1, KDG, K("L0b"))
     vcopy(A("e0b"), A("L0b"), 256, 0.5, K("L0b"), K("e0b"))
-    xr1k = xrep("xr1", T.xs[:, 1:W:S], [KX], "vs")
+    xr1k = xrep("xr1", T.xs[:, 1:W:S], [KX], XR1)
     if SG1[1]:
         vcopy(A("ndg"), A("ndi"), 256, 1, K("ndi"), K("ndg"))
         sact(T.dcod[:, 0:W:S], A("ndg"), AF.Exp, 256, K("ndg"), ["code"], bias=-MID / ALPHA, scale=1.0 / ALPHA)
-    vcopy(T.dgs[:, 0:W:S], A("ndi"), 256, 1, K("ndi"), [KDG])
-    run(home(1, c, "L0b", "e0b", "LEb", "r1b", T.xr1, xr1k, [KDG]) for c in range(NCH))
+    vcopy(T.dgs[:, 0:W:S], A("ndi"), 256, 1, K("ndi"), KDG)
+    run(home(1, c, "L0b", "LEb", "r1b", T.xr1, xr1k, KDG) for c in range(NCH))
     vcopy(A("ndf"), A("nd2"), 256, 1, K("nd2"), K("ndf"))
     sact(T.code2[:, 0:W:S], A("ndf"), AF.Exp, 256, K("ndf"), ["code2"], bias=-MID / ALPHA, scale=1.0 / ALPHA)
     vcopy(A("yd0"), A("ndi"), 256, 1, K("ndi"), K("yd0"))
     add("y", 0.1, lambda: g.sync.dma_start(T.yd[:, 0:L], A("yd0")), K("yd0"), (), (), "ld5", 16, 2.0)
     vcopy(A("d0f"), A("L0b"), L, 1, K("L0b"), K("d0f"))
-    tb = {"X": T.xs2, "kx": "xs2", "code": T.code2, "kc": "code2", "th": T.pt2[:, 0:1], "kth": "pt2", "nt": T.pt2[:, 1:2], "knt": "pt2",
+    tb = {"X": T.xs2, "kx": "xs2", "code": T.code2, "kc": "code2", "th": T.pt2, "kth": "pt2", "nt": T.pt2, "knt": "pt2",
           "GT": T.pk2[:, 0:128], "kgt": "pk2", "aG": T.pk2[:, 128:256], "kag": "pk2"}
-    run(walk(1, c, "LEb", "r1b", tb, T.xr1, xr1k) for c in range(NCH))
+    run(walk(1, c, "LEb", "r1b", "e0b", tb, T.xr1, xr1k) for c in range(NCH))
     vcopy(A("yef"), A("LF_1"), L, 1, K("LF_1"), K("yef"))
     add("y", 0.1, lambda: g.sync.dma_start(T.ye[:, :], A("yef")), K("yef"), (), (), "ld6", 16, 2.0)
     wt = [keep(1, h, "e0b") for h in (0, 1)]
-    finish(1, "yd1", "d0f", wt)
+    finish(1, "yd1", "d0f", "e0b", wt)
     add("y", 0.1, lambda: g.sync.dma_start(T.yd[:, L:2 * L], A("yd1")), K("yd1"), (), (), "ld7", 16, 2.0)
 
     order = schedule(ops, tiles, bankof)
@@ -495,13 +524,13 @@ def F(fn):
 
 
 PW = 0.01
-SKEW = 2.0
+SKEW = 1.4
 BONUS = {}
 
 
 def kind(o):
     n = o["n"]
-    return (o["e"], str(n[0] if isinstance(n, tuple) else n))
+    return "%s%d %s" % (o["e"], o["c"], n[0] if isinstance(n, tuple) else n)
 
 
 SEML = 0.1
@@ -529,15 +558,16 @@ def schedule(ops, tiles, bankof):
     fin = [0.0] * n
     free = {}
     order = []
+    rt = [0.0] * n
+    pri = [PW * (bl[k] - SKEW * ops[k]["c"] + BONUS.get(kind(ops[k]), 0.0)) for k in range(n)]
+    free["n"] = -1.0
     while ready:
         best = None
         for k in ready:
             o = ops[k]
-            st = free.get(o["e"], 0.0) if o["e"] != "n" else 0.0
-            for d in o["deps"]:
-                x = fin[d] + (SEML if ops[d]["e"] != o["e"] else 0.05)
-                if x > st:
-                    st = x
+            st = max(rt[k], free.get(o["e"], 0.0))
+            if best is not None and st - pri[k] > best[0][0]:
+                continue
             b = -1
             if k in tfirst:
                 cand = [(bfree[i][0], i) for i in range(8) if bank[i] is None]
@@ -545,7 +575,7 @@ def schedule(ops, tiles, bankof):
                     continue
                 f, b = min(cand)
                 st = max(st, f + SEML if f > 0 else 0.0)
-            key = (st - PW * (bl[k] - SKEW * o["c"] + BONUS.get(kind(o), 0.0)), k)
+            key = (st - pri[k], k)
             if best is None or key < best[0]:
                 best = (key, k, st, b)
         if best is None:
@@ -572,6 +602,9 @@ def schedule(ops, tiles, bankof):
                 bfree[bb] = (fin[k], k)
         for s in succ[k]:
             left[s] -= 1
+            x = fin[k] + (SEML if ops[s]["e"] != o["e"] else 0.05)
+            if x > rt[s]:
+                rt[s] = x
             if left[s] == 0:
                 ready.append(s)
     return order

from concourse.bass import DstId, RemoteDMATransfer
from concourse.mybir import dt, AluOpType, AxisListType, ActivationFunctionType

W, L, S, N = 2048, 256, 8, 8
NCH = 4
LC = L // NCH
CW = 16 * LC
ALPHA = 60.0
MID = 1023.5
BIGP = 8192.0
AL = AluOpType
AF = ActivationFunctionType

U_ = ["L0a", "L0b", "L0i", "LEa", "LEb", "LEi", "L1_0", "L1_1", "ndo", "ndi", "nd2"] + ["%s_%d" % (n, t) for n in ("L2", "L3", "L4", "LF") for t in (0, 1)]
H_ = ["e0b", "d0i", "wd", "mh"] + ["%s_%d" % (n, t) for n in ("h1", "m1", "g1", "h2", "h3", "h4", "hF", "m2", "m3", "m4") for t in (0, 1)]
F_ = ["d0f", "dS_0", "dS_1", "mq", "q", "ga", "yd0", "yd1", "yef", "ndf", "ndg"] + ["ln%d_%d" % (k, t) for k in (2, 3, 4) for t in (0, 1)]
B_ = ["x0", "xi", "r1a", "r1b", "r1i", "any"] + ["%s_%d" % (n, t) for n in ("r2", "r3", "r4", "bs", "sq", "ch", "go") for t in (0, 1)]
I_ = ["qi", "ni"]
POOLS = {"PU": (U_, "uint16"), "PH": (H_, "float16"), "PF": (F_, "float32"), "PB": (B_, "bfloat16"), "PI": (I_, "int32")}
SLOT = {}
SCRATCH = {}
for _p in POOLS:
    _names, _dt = POOLS[_p]
    SCRATCH[_p] = ("sbuf", [128, 256 * len(_names)], _dt)
    for _k, _n in enumerate(_names):
        SLOT[_n] = (_p, 256 * _k)
SCRATCH.update({
    "dgs": ("sbuf", [128, W], "int32"), "dgf": ("sbuf", [128, W], "float32"), "xs": ("sbuf", [128, W], "bfloat16"),
    "dcod": ("sbuf", [128, W], "bfloat16"), "xs2": ("sbuf", [128, W], "bfloat16"), "code2": ("sbuf", [128, W], "bfloat16"),
    "xr0": ("sbuf", [128, 16 * L], "bfloat16"), "xr1": ("sbuf", [128, 16 * L], "bfloat16"), "xrn": ("sbuf", [128, 16 * L], "bfloat16"),
    "zb": ("sbuf", [128, 32 * L], "bfloat16"), "ab": ("sbuf", [128, 32 * L], "bfloat16"), "gb": ("sbuf", [128, 32 * L], "bfloat16"),
    "gh": ("sbuf", [128, 16 * L], "float16"),
    "selb": ("sbuf", [128, 2048], "bfloat16"), "seln": ("sbuf", [128, 2048], "bfloat16"), "edb": ("sbuf", [128, 2048], "bfloat16"), "edh": ("sbuf", [128, 2048], "float16"),
    "onb": ("sbuf", [128, 256], "bfloat16"), "onf": ("sbuf", [128, 256], "float32"), "on16": ("sbuf", [128, 128], "float32"),
    "idb": ("sbuf", [128, 128], "bfloat16"), "idh": ("sbuf", [128, 128], "float16"), "idn": ("sbuf", [128, 128], "float16"), "idq": ("sbuf", [128, 128], "float16"), "idm": ("sbuf", [128, 128], "float16"),
    "id37": ("sbuf", [128, 128], "float16"), "idp": ("sbuf", [128, 128], "bfloat16"), "idnb": ("sbuf", [128, 128], "bfloat16"), "idf": ("sbuf", [128, 128], "float32"),
    "blk0": ("sbuf", [128, 128], "bfloat16"), "blk": ("sbuf", [128, 128], "bfloat16"),
    "dupf": ("sbuf", [128, 256], "float32"), "dupb": ("sbuf", [128, 256], "bfloat16"), "iop": ("sbuf", [128, 256], "float32"),
    "prow": ("sbuf", [128, 256], "bfloat16"), "rst": ("sbuf", [128, 256], "float32"),
    "pm": ("sbuf", [128, 512], "float32"), "eq": ("sbuf", [128, 256], "bfloat16"),
    "iq": ("sbuf", [128, 128], "float32"), "thi": ("sbuf", [128, 4], "int32"), "tii": ("sbuf", [128, 4], "int32"), "sgi": ("sbuf", [128, 4], "int32"),
    "tif": ("sbuf", [128, 4], "float32"), "sgf": ("sbuf", [128, 4], "float32"),
    "gq": ("sbuf", [128, 512], "float32"), "gj": ("sbuf", [128, 128], "bfloat16"),
    "pk": ("sbuf", [128, 256], "bfloat16"), "pk2": ("sbuf", [128, 256], "bfloat16"),
    "pt": ("sbuf", [128, 8], "float32"), "pt2": ("sbuf", [128, 8], "float32"),
    "asum": ("sbuf", [128, 8], "float32"), "acol": ("sbuf", [128, 8], "float32"),
})
for _k in range(8):
    SCRATCH["bank%d" % _k] = ("psum", [128, 512], "float32")
SEMAPHORES = ["cv", "cs", "cp", "cg", "lsem", "ltab", "rx", "rtab", "rpk", "rpt", "rnh", "rn2"] + ["re%d" % c for c in range(NCH)] + ["rr%d" % c for c in range(NCH)] + ["ld%d" % k for k in range(10)]

CY = 0.83e-3 * 1.2
RELU = {(1, 0), (1, 2), (2, 3), (3, 3)}
SG1 = ((1, 2), (0, 1))
RS = ()
CHS = True
EDV, XR0, XRN, XR1 = "ssvsssssssvsssvs", "ssv", "v", "vs"
GC = 1.5
HOP = 2.5


def rank_program(g, core, T, topo):
    rank = T.rank_of(core)
    if rank is None:
        return
    cores = T.cores
    ops, lastw, readers, tiles, own = [], {}, {}, [], {}
    bankof = {}
    cur = [0]
    ENG = {"v": g.vector, "s": g.scalar, "p": g.tensor, "g": g, "y": g.sync}
    CSEM = {"v": "cv", "s": "cs", "p": "cp", "g": "cg"}

    def add(eng, dur, fn, r=(), w=(), ps=(), sem=None, inc=1, lat=0.0, extra=(), boost=0.0):
        k = len(ops)
        deps = set(extra)
        keys_w = list(w) + [("ps", t) for t in ps]
        for x in r:
            if x in lastw:
                deps.add(lastw[x])
        for x in keys_w:
            if x in lastw:
                deps.add(lastw[x])
            deps.update(readers.get(x, ()))
        for x in r:
            readers.setdefault(x, []).append(k)
        for x in keys_w:
            lastw[x] = k
            readers[x] = []
        deps.discard(k)
        hard = set(extra)
        for x in list(r) + list(w):
            hard.update(own.get(("w", x), ()))
        for x in w:
            hard.update(own.get(("r", x), ()))
            own.setdefault(("w", x), []).append(k)
        for x in r:
            own.setdefault(("r", x), []).append(k)
        soft = set(d for d in deps if ops[d]["e"] == eng and d not in hard and ps)
        ops.append({"e": eng, "d": dur, "f": fn, "deps": deps, "ps": list(ps), "sem": sem, "inc": inc, "lat": lat, "c": cur[0], "soft": soft, "n": keys_w[0] if keys_w else "-"})
        for t in ps:
            tiles[t].append(k)
        return k

    def tile():
        tiles.append([])
        return len(tiles) - 1

    def ps(t):
        return T["bank%d" % bankof[t]]

    def rng(c):
        if c is None:
            return 0, L
        if c < 0:
            h = -1 - c
            return 128 * h, 128 * h + 128
        return LC * c, LC * c + LC

    def A(name, c=None):
        p, o = SLOT[name]
        a, b = rng(c)
        return T[p][:, o + a:o + b]

    def K(name, c=None):
        a, b = rng(c)
        return [(name, k) for k in range(a // LC, b // LC)]

    def nn(c):
        a, b = rng(c)
        return b - a

    def vt(n, f):
        return 0.04 + max(64, n * f) * CY

    def vcopy(out, in_, n, f, r, w, p=()):
        return add("v", vt(n, f), lambda: g.vector.tensor_copy(R(out), R(in_)), r, w, p)

    def R(x):
        return x[0]() if isinstance(x, tuple) else x

    def vts(out, in0, s1, s2, o0, o1, n, f, r, w, p=()):
        def em():
            i0 = R(in0)
            if o1 is None:
                return g.vector.tensor_scalar(out, i0, s1, None, o0)
            return g.vector.tensor_scalar(out, i0, s1, s2, o0, o1)
        return add("v", vt(n, f), em, r, w, p)

    def vtt(out, in0, in1, op, n, f, r, w, p=()):
        return add("v", vt(n, f), lambda: g.vector.tensor_tensor(out, R(in0), R(in1), op), r, w, p)

    def sact(out, in_, func, n, r, w, p=(), bias=0.0, scale=1.0, acc=None):
        def em():
            i0 = R(in_)
            if acc is not None:
                return g.scalar.activation(out, i0, func, bias=bias, scale=scale, accum_out=acc)
            return g.scalar.activation(out, i0, func, bias=bias, scale=scale)
        return add("s", 0.08 + n * CY, em, r, w, p)

    def mm(lst, cyc, r, p):
        def em():
            out = None
            for (a, b, lhs, rhs, st, sp) in lst:
                out = g.tensor.matmul(ps(p)[:, a:b], lhs, rhs, st, sp)
            return out
        return add("p", 0.03 + cyc * 0.6e-3, em, r, (), (p,))

    def load(eng, buf, src, sem, lat):
        q = g.sync if eng == "y" else g.scalar
        return add(eng, 0.1, lambda: q.dma_start(buf, src), (), [(sem, "ld")], (), sem, 16, lat)

    load("y", T.dgs[:, 0:W // 2], T.dg[:, 0:W // 2], "ld1", 4.5)
    load("y", T.dgs[:, W // 2:W], T.dg[:, W // 2:W], "ld8", 7.0)
    load("y", T.xs[:, :], T.xv[:, :], "ld0", 9.0)
    load("y", T.thi[:, 0:1], T.th[:, :], "ld4", 9.5)
    load("y", T.tii[:, 0:3], T.ti[:, :], "ld2", 9.5)
    load("y", T.sgi[:, 0:3], T.sg[:, :], "ld3", 9.5)
    KX, KDG = ("ld0", "ld"), [("ld1", "ld"), ("ld8", "ld")]

    add("v", vt(256, 0.5), lambda: g.vector.memset(T.onb[:, :], 1.0), (), ["onb"])
    add("v", vt(256, 1), lambda: g.vector.memset(T.onf[:, :], 1.0), (), ["onf"])
    add("v", vt(2048, 0.5), lambda: g.vector.memset(T.edb[:, :], 0.0), (), ["edb0"])
    add("v", vt(2048, 0.5), lambda: g.vector.memset(T.selb[:, :], 0.0), (), ["selb0"])
    add("g", 0.4, lambda: g.affine_select(T.idb[:, :], T.onb[:, 0:128], [[-1, 128]], AL.is_equal, 0.0, 0, 1), ["onb"], ["idb"])
    add("g", 0.4, lambda: g.affine_select(T.blk0[:, :], T.onb[:, 0:128], [[-16, 8], [0, 16]], AL.is_ge, 0.0, 0, 1), ["onb"], ["blk0"])
    add("g", 0.4, lambda: g.affine_select(T.blk[:, :], T.blk0[:, :], [[16, 8], [0, 16]], AL.is_ge, 0.0, 15, -1), ["blk0"], ["blk"])
    add("g", 0.4, lambda: g.iota(T.iq[:, :], [[0, 8], [1, 16]], 0, 0, allow_small_or_imprecise_dtypes=True), (), ["iq"])
    add("g", 0.6, lambda: g.affine_select(T.dupf[:, :], T.onf[:, :], [[-16, 8], [0, 2], [-1, 16]], AL.is_equal, 0.0, 0, 1), ["onf"], ["dupf"])
    add("g", 0.6, lambda: g.iota(T.iop[:, :], [[0, 8], [0, 2], [1, 16]], 0, 0, allow_small_or_imprecise_dtypes=True), (), ["iop"])
    for p in range(16):
        def cp(p=p):
            if EDV[p] == "v":
                return g.vector.tensor_copy(T.edb[:, p * 128 + p:(p + 1) * 128:16], T.idb[:, p:128:16])
            return g.scalar.activation(T.edb[:, p * 128 + p:(p + 1) * 128:16], T.idb[:, p:128:16], AF.Copy)
        add(EDV[p], vt(8, 1), cp, ["idb", "edb0"], [("edb", p)])
    KED = [("edb", p) for p in range(16)]
    vcopy(T.edh[:, :], T.edb[:, :], 2048, 0.5, KED, ["edh"])
    for p in range(16):
        def cp2(p=p):
            return g.scalar.activation(T.selb[:, p * 128 + p:(p + 1) * 128:16], T.blk[:, 0:128:16], AF.Copy)
        add("s", 0.08 + 8 * CY, cp2, ["blk", "selb0"], [("selb", p)])
    KSEL = [("selb", p) for p in range(16)]
    if RELU:
        vts(T.seln[:, :], T.selb[:, :], -1.0, None, AL.mult, None, 2048, 0.5, KSEL, ["seln"])
    vcopy(T.idh[:, :], T.idb[:, :], 128, 0.5, ["idb"], ["idh"])
    vts(T.idn[:, :], T.idb[:, :], -1.0, None, AL.mult, None, 128, 0.5, ["idb"], ["idn"])
    vts(T.id37[:, :], T.idb[:, :], 37.0, None, AL.mult, None, 128, 0.5, ["idb"], ["id37"])
    vts(T.idp[:, :], T.idb[:, :], BIGP / 2, None, AL.mult, None, 128, 0.5, ["idb"], ["idp"])
    vts(T.idq[:, :], T.idb[:, :], 0.5, None, AL.mult, None, 128, 0.5, ["idb"], ["idq"])
    vts(T.idm[:, :], T.idb[:, :], -0.5, None, AL.mult, None, 128, 0.5, ["idb"], ["idm"])

    def xrep(buf, src, rk, engs):
        keys = []
        for p in range(16):
            e = engs[p % len(engs)]
            o = T[buf][:, p:16 * L:16]
            key = (buf, p)
            keys.append(key)
            if e == "v":
                vcopy(o, src, 256, 0.5, rk, [key])
            else:
                sact(o, src, AF.Copy, 256, rk, [key])
        return keys

    xr0k = xrep("xr0", T.xs[:, 0:W:S], [KX], XR0)
    vcopy(A("x0"), T.xs[:, 0:W:S], 256, 0.5, [KX], K("x0"))
    for h in (0, 1):
        vcopy(A("L0a", -1 - h), T.dgs[:, h * W // 2:(h + 1) * W // 2:S], 128, 1, [KDG[h]], K("L0a", -1 - h))

    vcopy(T.tif[:, 0:3], T.tii[:, 0:3], 3, 1, [("ld2", "ld")], ["tif"])
    vcopy(T.sgf[:, 0:3], T.sgi[:, 0:3], 3, 1, [("ld3", "ld")], ["sgf"])
    for j, (a, b) in enumerate(((-1.0, 0.5), (-1.0, 0.5 + BIGP / 2), (1.0, 0.0), (1.0, -BIGP / 2))):
        vts(T.pt[:, j:j + 1], T.thi[:, 0:1], a, b, AL.mult, AL.add, 1, 1, [("ld4", "ld")], ["ptk"])
    PTK = ["ptk"]

    def dest(r):
        return cores[r % N]

    def send(dsts, names_in, names_out, sem, dur, rd, after=(), lsem="lsem"):
        trs, tot = [], 0
        pieces = len(names_in)
        for k in range(pieces):
            d = dsts[k]
            rid, pid = topo.addr(d, core)
            es = topo.engines(core, d)
            n = 1
            while 2 * n * pieces <= min(len(es), 8):
                n *= 2
            m = sum(1 << e for e in es[k * n:(k + 1) * n])
            trs.append((DstId(rid=rid, pnc=pid), m, names_in[k], names_out[k], sem[k]))
            tot += n
        if lsem == "lsem":
            cnt["l"] += tot

        def em():
            return g.remote_dma_fused([RemoteDMATransfer(dst_ids=[a], dma_engine_mask=m, remote_sem=T.sem[s_], src=i, dst=o)
                                       for (a, m, i, o, s_) in trs], local_sem=T.sem[lsem])
        return add("g", dur, em, rd, (), (), "-", 0, 0.0, after)

    cnt = {"l": 0}

    def recv(sem, val, lat, after, keys):
        return add("n", 0.0, None, (), keys, (), sem, val, lat, [after])

    s1 = dest(rank + 1)
    k = send([s1, s1], [A("x0"), A("L0a")], [A("xi"), A("L0i")], ["rx", "rx"], 1.5, K("x0") + K("L0a"))
    recv("rx", 8, HOP, k, K("xi") + K("L0i"))

    par = {}

    def bufpair(buf, c):
        n = par.get((buf, c), 0)
        par[(buf, c)] = n + 1
        o = (n % 2) * 16 * L + c * CW
        return o, (buf, n % 2, c)

    GT_ = 0.06 + CW * GC * CY

    def diag(src, key, ed, kd, p, off=0, o0=0):
        mm([(off, off + LC, ed[:, q * 128:(q + 1) * 128], src[:, o0 + q:o0 + CW:16], q == 0, q == 15) for q in range(16)], CW, [key] + kd, p)

    def view(X, kx, lst, kl, xr, kxr, c, st):
        zo, zk = bufpair("zb", c)
        add("v", GT_, lambda: g.vector.tensor_tensor(T.zb[:, zo:zo + CW], X[:, :].indirect(lst), xr[:, c * CW:(c + 1) * CW], AL.subtract),
            [kx] + kl + kxr, [zk])
        ao, ak = bufpair("ab", c)
        if (st, c) in RELU:
            vts(T.ab[:, ao:ao + CW], T.zb[:, zo:zo + CW], 0.0, 2.0, AL.max, AL.mult, CW, 0.5, [zk], [ak])
        else:
            sact(T.ab[:, ao:ao + CW], T.zb[:, zo:zo + CW], AF.Abs, CW, [zk], [ak])
        return zo, zk, ao, ak

    def dist(v4, st, c, p, off, pen=None):
        zo, zk, ao, ak = v4
        two = (st, c) in RELU
        if two:
            mm([(off, off + LC, T.seln[:, q * 128:(q + 1) * 128], T.zb[:, zo + q:zo + CW:16], q == 0, False) for q in range(16)], CW, [zk, "seln"], p)
        mm([(off, off + LC, T.selb[:, q * 128:(q + 1) * 128], T.ab[:, ao + q:ao + CW:16], q == 0 and not two, q == 15 and pen is None) for q in range(16)],
           CW, [ak] + KSEL, p)
        if pen is not None:
            mm([(off, off + LC, T.idp[:, :], pen[0], False, True)], LC, pen[1] + ["idp"], p)

    def rest(k, c, rk, q, th, kth):
        j = 1 if (k - 1) in RS else 0
        if k in RS:
            sact(A(rk, c), F(lambda: ps(q)[:, 0:LC]), AF.Sign, LC, [kth], K(rk, c), (q,), bias=th[:, j:j + 1])
        else:
            vts(A(rk, c), F(lambda: ps(q)[:, 0:LC]), th[:, 2 + j:3 + j], 2.0, AL.is_ge, AL.mult, LC, 1, [kth], K(rk, c), (q,))

    def home(t, c, L0, L1, r1, xr, kxr, kdg):
        p = tile()
        if c in SG1[t]:
            go, gk = bufpair("gb", c)
            add("s", GT_, lambda: g.scalar.activation(T.gb[:, go:go + CW], T.dcod[:, :].indirect(A(L0, c)), AF.Copy), ["code"] + K(L0, c), [gk])
            diag(T.gb, gk, T.edb, KED, p, 0, go)
            lk = "ln2_%d" % t
            sact(A(lk, c), F(lambda: ps(p)[:, 0:LC]), AF.Ln, LC, (), K(lk, c), (p,))
            vts(A(L1, c), A(lk, c), ALPHA, MID + 0.25, AL.mult, AL.add, LC, 1, K(lk, c), K(L1, c))
        else:
            add("v", GT_, lambda: g.vector.tensor_copy(T.gh[:, c * CW:(c + 1) * CW], T.dgs[:, :].indirect(A(L0, c))), kdg + K(L0, c), [("gh", c)])
            diag(T.gh, ("gh", c), T.edh, ["edh"], p, 0, c * CW)
            vcopy(A(L1, c), F(lambda: ps(p)[:, 0:LC]), LC, 1, (), K(L1, c), (p,))
        yield
        q = tile()
        dist(view(T.xs, KX, A(L1, c), K(L1, c), xr, kxr, c, 1), 1, c, q, 0)
        rest(1, c, r1, q, T.pt, "ptk")
        yield

    def walk(t, c, L1, r1, e0, tb, xr, kxr):
        X, kx, code, kc, th, kth = tb["X"], tb["kx"], tb["code"], tb["kc"], tb["th"], tb["kth"]
        h1 = "h1_%d" % t
        m1 = "m1_%d" % t
        vcopy(A(h1, c), A(L1, c), LC, 0.5, K(L1, c), K(h1, c))
        lst, hp, rp, ms = L1, h1, r1, [m1]
        for k in (2, 3, 4):
            Lk, hk, lk, rk, mk = ["%s%d_%d" % (n, k, t) for n in ("L", "h", "ln", "r", "m")]
            go, gk = bufpair("gb", c)

            def gat(go=go, lst=lst):
                return g.scalar.activation(T.gb[:, go:go + CW], code[:, :].indirect(A(lst, c)), AF.Copy)
            add("s", GT_, gat, [kc] + K(lst, c), [gk])
            p = tile()
            diag(T.gb, gk, T.edb, KED, p, 0, go)
            sact(A(lk, c), F(lambda p=p: ps(p)[:, 0:LC]), AF.Ln, LC, (), K(lk, c), (p,))
            vts(A(Lk, c), A(lk, c), ALPHA, MID + 0.25, AL.mult, AL.add, LC, 1, K(lk, c), K(Lk, c))
            vcopy(A(hk, c), A(Lk, c), LC, 0.5, K(Lk, c), K(hk, c))
            q = tile()
            mm([(LC, 2 * LC, T.idh[:, :], A(hp, c), True, False), (LC, 2 * LC, T.idn[:, :], A(hk, c), False, True)], 2 * LC,
               K(hp, c) + K(hk, c) + ["idh", "idn"], q)
            if k == 2:
                mm([(2 * LC, 3 * LC, T.idh[:, :], A(e0, c), True, False), (2 * LC, 3 * LC, T.idn[:, :], A(h1, c), False, True)], 2 * LC,
                   K(e0, c) + K(h1, c) + ["idh", "idn"], q)
                vtt(A(m1, c), A(r1, c), F(lambda q=q: ps(q)[:, 2 * LC:3 * LC]), AL.mult, LC, 1, K(r1, c), K(m1, c), (q,))
            dist(view(X, kx, A(Lk, c), K(Lk, c), xr, kxr, c, k), k, c, q, 0, (A(rp, c), K(rp, c)))
            rest(k, c, rk, q, th, kth)
            vtt(A(mk, c), A(rk, c), F(lambda q=q: ps(q)[:, LC:2 * LC]), AL.mult, LC, 1, K(rk, c), K(mk, c), (q,))
            lst, hp, rp = Lk, hk, rk
            ms.append(mk)
            yield
        LF, hF = "LF_%d" % t, "hF_%d" % t
        p = tile()
        hs = [e0, h1] + ["h%d_%d" % (k, t) for k in (2, 3, 4)]
        seq = [(T.idh, hp)] + [(T.idq, x) for x in ms]
        for k in RS:
            seq += [(T.idq, hs[k - 1]), (T.idm, hs[k])]
        mm([(0, LC, w[:, :], A(x, c), i == 0, i == len(seq) - 1) for i, (w, x) in enumerate(seq)], len(seq) * LC,
           sum([K(x, c) for w, x in seq], []) + ["idq", "idh", "idm"], p)
        vcopy(A(LF, c), F(lambda: ps(p)[:, 0:LC]), LC, 1, (), K(LF, c), (p,))
        zo, zk, ao, ak = v4 = view(X, kx, A(LF, c), K(LF, c), xr, kxr, c, 5)
        vcopy(A(hF, c), A(LF, c), LC, 0.5, K(LF, c), K(hF, c))
        p2 = tile()
        diag(T.zb, zk, T.edb, KED, p2, LC, zo)
        bs, sq, ch, dS = "bs_%d" % t, "sq_%d" % t, "ch_%d" % t, "dS_%d" % t
        sact(A(bs, c), F(lambda: ps(p2)[:, LC:2 * LC]), AF.Sign, LC, (), K(bs, c), (p2,), bias=-0.5)
        p3 = tile()
        dist(v4, 5, c, p3, 0)
        sact(A(dS, c), F(lambda: ps(p3)[:, 0:LC]), AF.Copy, LC, (), K(dS, c), (p3,))
        p4 = tile()
        mm([(0, LC, tb["GT"], A(bs, c), True, True)], LC, K(bs, c) + [tb["kgt"]], p4)
        sact(A(sq, c), F(lambda: ps(p4)[:, 0:LC]), AF.Square, LC, (), K(sq, c), (p4,))
        p5 = tile()
        mm([(0, LC, tb["aG"], A(sq, c), True, True), (LC, 2 * LC, T.blk[:, :], A(sq, c), True, True)], 2 * LC, K(sq, c) + [tb["kag"], "blk"], p5)
        if CHS:
            sact(A(ch, c), F(lambda: ps(p5)[:, 0:LC]), AF.Sign, LC, [tb["knt"]], K(ch, c), (p5,), bias=tb["nt"][:, 4:5])
        else:
            vts(A(ch, c), F(lambda: ps(p5)[:, 0:LC]), tb["nt"][:, 5:6], None, AL.is_gt, None, LC, 1, [tb["knt"]], K(ch, c), (p5,))
        sact(A("any", c), F(lambda: ps(p5)[:, LC:2 * LC]), AF.Sign, LC, (), K("any", c) + [("asum", t, c)], (p5,), bias=-16.0,
             acc=T.asum[:, 4 * t + c:4 * t + c + 1])
        yield

    def keep(t, h, D0h):
        c = -1 - h
        dS, ch, hF, go = "dS_%d" % t, "ch_%d" % t, "hF_%d" % t, "go_%d" % t
        p = tile()
        mm([(0, 256, A(dS, c), T.dupf[:, :], True, False), (0, 256, T.onb[:, 0:128], T.prow[:, :], False, False)],
           1024 + 256, K(dS, c) + ["dupf", "onb", "prow"], p)
        mm([(0, 256, A(ch, c), T.dupb[:, :], False, True)], 256, K(ch, c) + ["dupb"], p)
        add("v", vt(256, 1), lambda: g.vector.tensor_tensor_scan(T.pm[:, 256 * h:256 * h + 256], T.rst[:, :], ps(p)[:, 0:256], 0.0, AL.mult, AL.min),
            ["rst"], [("pm", h)], (p,))
        for x in range(8):
            vtt(T.eq[:, 128 * h + 16 * x:128 * h + 16 * x + 16], T.pm[:, 256 * h + 32 * x + 16:256 * h + 32 * x + 32],
                F(lambda x=x: ps(p)[:, 32 * x + 16:32 * x + 32]), AL.is_equal, 16, 1, [("pm", h)], [("eq", h, x)], (p,))
        q = tile()
        mm([(0, 128, T.id37[:, :], A(hF, c), True, False), (0, 128, T.idf[:, :], A(dS, c), False, True)],
           640, K(hF, c) + K(dS, c) + ["id37", "idf"], q)
        u = tile()
        mm([(0, 128, T.idb[:, :], A(ch, c), True, False)], 128, K(ch, c) + ["idb"], u)
        mm([(0, 128, T.eq[:, 128 * h:128 * h + 128], T.idnb[:, :], False, True)], 128, [("eq", h, x) for x in range(8)] + ["idnb"], u)
        return q, u

    def finish(t, out, D0f, D0h, wt):
        p = tile()
        mm([(0, 1, T.on16[:, :], T.asum[:, 4 * t + c:4 * t + c + 1], c == 0, c == NCH - 1) for c in range(NCH)], 4 * 4 * 64,
           [("asum", t, c) for c in range(NCH)] + ["on16"], p)
        vcopy(T.acol[:, t:t + 1], F(lambda: ps(p)[:, 0:1]), 1, 1, (), [("acol", t)], (p,))
        for c in (-1, -2):
            q, u = wt[-1 - c]
            vts(A("qi", c), F(lambda q=q: ps(q)[:, 0:128]), T.acol[:, t:t + 1], None, AL.add, None, 128, 1, [("acol", t)], K("qi", c), (q,))
            vts(A("ni", c), A("qi", c), W - 1, None, AL.bitwise_and, None, 128, 1, K("qi", c), K("ni", c))
            vtt(A("wd", c), A("ni", c), A(D0f, c), AL.subtract, 128, 2, K("ni", c) + K(D0f, c), K("wd", c))
            vtt(A("mh", c), A("wd", c), F(lambda u=u: ps(u)[:, 0:128]), AL.mult, 128, 1, K("wd", c), K("mh", c), (u,))
            v = tile()
            mm([(0, 128, T.idh[:, :], A(D0h, c), True, False), (0, 128, T.idh[:, :], A("mh", c), False, True)], 256, K(D0h, c) + K("mh", c) + ["idh"], v)
            vcopy(A(out, c), F(lambda v=v: ps(v)[:, 0:128]), 128, 1, (), K(out, c), (v,))

    def run(gens):
        gens = list(enumerate(gens))
        while gens:
            nxt = []
            for c, x in gens:
                cur[0] = c
                try:
                    next(x)
                    nxt.append((c, x))
                except StopIteration:
                    pass
            gens = nxt
        cur[0] = 0

    for h in (0, 1):
        a, b = h * W // 2, (h + 1) * W // 2
        vcopy(T.dgf[:, a:b], T.dgs[:, a:b], W // 2, 1, [KDG[h]], [("dgf", h)])
        sact(T.dcod[:, a:b], T.dgf[:, a:b], AF.Exp, W // 2, [("dgf", h)], ["code"], bias=-MID / ALPHA, scale=1.0 / ALPHA)

    run(home(0, c, "L0a", "LEa", "r1a", T.xr0, xr0k, KDG) for c in range(NCH))
    for c in range(NCH):
        last = send([s1], [A("LEa", c)], [A("LEi", c)], ["re%d" % c], 1.0, K("LEa", c))
        recv("re%d" % c, 8, HOP, last, K("LEi", c))
    for c in range(NCH):
        last = send([s1], [A("r1a", c)], [A("r1i", c)], ["rr%d" % c], 1.0, K("r1a", c))
        recv("rr%d" % c, 8, HOP, last, K("r1i", c))

    for k in range(3):
        vts(T.gq[:, 128 * k:128 * k + 128], T.iq[:, :], T.tif[:, k:k + 1], T.sgf[:, k:k + 1], AL.is_equal, AL.mult, 128, 1, ["iq", "tif", "sgf"], [("gq", k)])
    vtt(T.gq[:, 384:512], T.gq[:, 0:128], T.gq[:, 128:256], AL.add, 128, 2, [("gq", 0), ("gq", 1)], [("gq", 3)])
    vtt(T.gq[:, 0:128], T.gq[:, 384:512], T.gq[:, 256:384], AL.add, 128, 2, [("gq", 3), ("gq", 2)], [("gq", 0)])
    vtt(T.gj[:, :], T.gq[:, 0:128], T.blk[:, :], AL.mult, 128, 2, [("gq", 0), "blk"], ["gj"])
    sact(T.pk[:, 128:256], T.gj[:, :], AF.Abs, 128, ["gj"], ["pkA"])
    p0 = tile()
    mm([(0, 128, T.gj[:, :], T.idb[:, :], True, True), (128, 129, T.pk[:, 128:256], T.onb[:, 0:1], True, True)], 192, ["gj", "idb", "pkA", "onb"], p0)
    sact(T.pk[:, 0:128], F(lambda: ps(p0)[:, 0:128]), AF.Copy, 128, (), ["pkG"], (p0,))
    vts(T.pt[:, 4:5], F(lambda: ps(p0)[:, 128:129]), -1.0, None, AL.mult, None, 1, 1, (), ["ptn"], (p0,))
    vcopy(T.pt[:, 5:6], F(lambda: ps(p0)[:, 128:129]), 1, 1, (), ["ptn"], (p0,))
    xrnk = xrep("xrn", A("xi"), K("xi"), XRN)
    vcopy(A("d0i"), A("L0i"), L, 0.5, K("L0i"), K("d0i"))
    vcopy(A("d0f"), A("L0i"), L, 1, K("L0i"), K("d0f"))

    h2 = dest(rank - 2)
    k = send([h2, h2], [T.xs[:, :], T.dcod[:, :]], [T.xs2[:, :], T.code2[:, :]], ["rtab", "rtab"], 1.0, [KX, "code"], (last,), "ltab")
    add("n", 0.0, None, ["code"], (), (), "ltab", 8, 25.0, [k])
    recv("rtab", 8, 25.0, k, ["xs2", "code2"])
    k = send([h2], [T.pk[:, :]], [T.pk2[:, :]], ["rpk"], 1.0, ["pkA", "pkG"], (k,))
    recv("rpk", 8, 25.0, k, ["pk2"])
    k = send([h2], [T.pt[:, 0:6]], [T.pt2[:, 0:6]], ["rpt"], 1.0, PTK + ["ptn"], (k,))
    recv("rpt", 8, 25.0, k, ["pt2"])

    vcopy(T.idf[:, :], T.idb[:, :], 128, 1, ["idb"], ["idf"])
    vts(T.dupb[:, :], T.dupf[:, :], -BIGP, None, AL.mult, None, 256, 1, ["dupf"], ["dupb"])
    vts(T.prow[:, :], T.iop[:, :], 1.0 / 4096, 1.0 / 8192, AL.mult, AL.add, 256, 1, ["iop"], ["prow"])
    add("v", vt(256, 1), lambda: g.vector.memset(T.rst[:, :], 1.0), (), ["rst"])
    add("v", vt(8, 1), lambda: g.vector.memset(T.rst[:, 0:256:32], 0.0), (), ["rst"])
    vts(T.idnb[:, :], T.idb[:, :], -1.0, None, AL.mult, None, 128, 0.5, ["idb"], ["idnb"])
    add("v", vt(128, 1), lambda: g.vector.memset(T.on16[:, :], 1.0 / 16), (), ["on16"])

    tb = {"X": T.xs, "kx": KX, "code": T.dcod, "kc": "code", "th": T.pt, "kth": "ptk", "nt": T.pt, "knt": "ptn",
          "GT": T.pk[:, 0:128], "kgt": "pkG", "aG": T.pk[:, 128:256], "kag": "pkA"}
    run(walk(0, c, "LEi", "r1i", "d0i", tb, T.xrn, xrnk) for c in range(NCH))
    wt = [keep(0, h, "d0i") for h in (0, 1)]
    finish(0, "ndo", "d0f", "d0i", wt)
    d1, d2 = dest(rank - 1), dest(rank - 3)
    k = send([d1], [A("ndo")], [A("ndi")], ["rnh"], 1.0, K("ndo"))
    recv("rnh", 8, HOP, k, K("ndi"))
    k = send([d2], [A("ndo")], [A("nd2")], ["rn2"], 1.0, K("ndo"), (k,))
    recv("rn2", 8, HOP, k, K("nd2"))

    vcopy(A("L0b"), T.dgs[:, 1:W:S], 256, 1, KDG, K("L0b"))
    vcopy(A("e0b"), A("L0b"), 256, 0.5, K("L0b"), K("e0b"))
    xr1k = xrep("xr1", T.xs[:, 1:W:S], [KX], XR1)
    if SG1[1]:
        vcopy(A("ndg"), A("ndi"), 256, 1, K("ndi"), K("ndg"))
        sact(T.dcod[:, 0:W:S], A("ndg"), AF.Exp, 256, K("ndg"), ["code"], bias=-MID / ALPHA, scale=1.0 / ALPHA)
    vcopy(T.dgs[:, 0:W:S], A("ndi"), 256, 1, K("ndi"), KDG)
    run(home(1, c, "L0b", "LEb", "r1b", T.xr1, xr1k, KDG) for c in range(NCH))
    vcopy(A("ndf"), A("nd2"), 256, 1, K("nd2"), K("ndf"))
    sact(T.code2[:, 0:W:S], A("ndf"), AF.Exp, 256, K("ndf"), ["code2"], bias=-MID / ALPHA, scale=1.0 / ALPHA)
    vcopy(A("yd0"), A("ndi"), 256, 1, K("ndi"), K("yd0"))
    add("y", 0.1, lambda: g.sync.dma_start(T.yd[:, 0:L], A("yd0")), K("yd0"), (), (), "ld5", 16, 2.0)
    vcopy(A("d0f"), A("L0b"), L, 1, K("L0b"), K("d0f"))
    tb = {"X": T.xs2, "kx": "xs2", "code": T.code2, "kc": "code2", "th": T.pt2, "kth": "pt2", "nt": T.pt2, "knt": "pt2",
          "GT": T.pk2[:, 0:128], "kgt": "pk2", "aG": T.pk2[:, 128:256], "kag": "pk2"}
    run(walk(1, c, "LEb", "r1b", "e0b", tb, T.xr1, xr1k) for c in range(NCH))
    vcopy(A("yef"), A("LF_1"), L, 1, K("LF_1"), K("yef"))
    add("y", 0.1, lambda: g.sync.dma_start(T.ye[:, :], A("yef")), K("yef"), (), (), "ld6", 16, 2.0)
    wt = [keep(1, h, "e0b") for h in (0, 1)]
    finish(1, "yd1", "d0f", "e0b", wt)
    add("y", 0.1, lambda: g.sync.dma_start(T.yd[:, L:2 * L], A("yd1")), K("yd1"), (), (), "ld7", 16, 2.0)

    order = schedule(ops, tiles, bankof)
    emit(g, T, ENG, CSEM, ops, order, cnt["l"])


def F(fn):
    return (fn,)


PW = 0.01
SKEW = 1.4
BONUS = {}


def kind(o):
    n = o["n"]
    return "%s%d %s" % (o["e"], o["c"], n[0] if isinstance(n, tuple) else n)


SEML = 0.1


def schedule(ops, tiles, bankof):
    n = len(ops)
    succ = [[] for _ in range(n)]
    for k in range(n):
        for d in ops[k]["deps"]:
            succ[d].append(k)
    bl = [0.0] * n
    for k in range(n - 1, -1, -1):
        o = ops[k]
        bl[k] = o["d"] + o["lat"] + max([bl[s] for s in succ[k]] + [0.0])
    tfirst = {}
    for t, lst in enumerate(tiles):
        if lst:
            tfirst[lst[0]] = t
    tleft = [len(x) for x in tiles]
    bank = [None] * 8
    bfree = [(0.0, None)] * 8
    left = [len(o["deps"]) for o in ops]
    ready = [k for k in range(n) if left[k] == 0]
    fin = [0.0] * n
    free = {}
    order = []
    rt = [0.0] * n
    pri = [PW * (bl[k] - SKEW * ops[k]["c"] + BONUS.get(kind(ops[k]), 0.0)) for k in range(n)]
    free["n"] = -1.0
    while ready:
        best = None
        for k in ready:
            o = ops[k]
            st = max(rt[k], free.get(o["e"], 0.0))
            if best is not None and st - pri[k] > best[0][0]:
                continue
            b = -1
            if k in tfirst:
                cand = [(bfree[i][0], i) for i in range(8) if bank[i] is None]
                if not cand:
                    continue
                f, b = min(cand)
                st = max(st, f + SEML if f > 0 else 0.0)
            key = (st - pri[k], k)
            if best is None or key < best[0]:
                best = (key, k, st, b)
        if best is None:
            raise ValueError("no free PSUM bank")
        _, k, st, b = best
        o = ops[k]
        ready.remove(k)
        if b >= 0:
            t = tfirst[k]
            bankof[t] = b
            bank[b] = t
            if bfree[b][1] is not None:
                o["deps"].add(bfree[b][1])
        if o["e"] != "n":
            free[o["e"]] = st + o["d"]
        fin[k] = st + o["d"] + o["lat"]
        o["st"] = st
        order.append(k)
        for t in o["ps"]:
            tleft[t] -= 1
            if tleft[t] == 0:
                bb = bankof[t]
                bank[bb] = None
                bfree[bb] = (fin[k], k)
        for s in succ[k]:
            left[s] -= 1
            x = fin[k] + (SEML if ops[s]["e"] != o["e"] else 0.05)
            if x > rt[s]:
                rt[s] = x
            if left[s] == 0:
                ready.append(s)
    return order


def emit(g, T, ENG, CSEM, ops, order, nlocal):
    count = {"v": 0, "s": 0, "p": 0, "g": 0}
    known = {e: {} for e in ENG}
    done = {}
    waited = {}
    for k in order:
        o = ops[k]
        e = o["e"]
        if e == "n":
            done[k] = (o["sem"], o["inc"], {})
            continue
        q = ENG[e]
        need = {}
        imp = dict(known[e])
        for d in o["deps"]:
            if done[d] is None or d in o["soft"]:
                continue
            if e == "p" and ops[d]["e"] == "p":
                continue
            s, v, _i = done[d]
            if known[e].get(s, 0) < v and need.get(s, (0, 0))[0] < v:
                need[s] = (v, d)
        for s in list(need):
            v, d = need[s]
            for s2 in need:
                if s2 != s and done[need[s2][1]][2].get(s, 0) >= v:
                    del need[s]
                    break
        for s in need:
            v, d = need[s]
            q.wait_ge(T.sem[s], v)
            waited[s] = max(waited.get(s, 0), v)
            for a, b in done[d][2].items():
                if known[e].get(a, 0) < b:
                    known[e][a] = b
            known[e][s] = max(known[e].get(s, 0), v)
        inst = o["f"]()
        if o["sem"] == "-":
            done[k] = None
            continue
        if o["sem"] is None:
            count[e] += 1
            s, v = CSEM[e], count[e]
            inst.then_inc(T.sem[s], 1)
        else:
            s, v = o["sem"], o["inc"]
            inst.then_inc(T.sem[s], v)
        done[k] = (s, v, dict(known[e]))
    total = {CSEM[e]: count[e] for e in count if count[e]}
    total["lsem"] = nlocal
    for k in order:
        o = ops[k]
        if o["sem"] not in (None, "-"):
            total[o["sem"]] = o["inc"]
    for s in total:
        if waited.get(s, 0) < total[s]:
            g.wait_ge(T.sem[s], total[s])
